import numpy as np
import ml_dtypes


def mxq(x, axis, fmt="e4m3"):
    dtype, down = {"e4m3": (ml_dtypes.float8_e4m3fn, 7), "e5m2": (ml_dtypes.float8_e5m2, 14)}[fmt]
    v = np.moveaxis(np.asarray(x, np.float32).astype(ml_dtypes.bfloat16).astype(np.float64), axis, -1)
    blocks = v.reshape(v.shape[:-1] + (-1, 32))
    amax = np.abs(blocks).max(-1, keepdims=True)
    byte = np.maximum(np.where(amax > 0, np.frexp(amax)[1] - 1 + 127, 0) - down, 1)
    scale = np.exp2(byte - 127.0)
    codes = (blocks / scale).astype(np.float32).astype(dtype).astype(np.float64)
    return np.moveaxis((codes * scale).reshape(v.shape), -1, axis)


WIDE = False


def mx_kscale(k):
    if not WIDE:
        return np.ones(k)
    levels = np.array([10, -10, 5, -5, 0])
    if k % 512:
        return np.exp2(np.random.permutation(np.resize(levels, k // 32))).repeat(32)
    a = np.empty((k // 512, 16))
    for p in range(k // 512):
        a[p, :8] = np.random.permutation(np.resize(levels, 8))
        for g in range(8):
            far = levels[np.abs(levels - a[p, g]) >= 10]
            a[p, g + 8] = far[np.random.randint(len(far))]
    return np.exp2(a.ravel()).repeat(32)


def f64(x):
    return np.asarray(x).astype(np.float64)


def striped(idx):
    return np.tile(idx.reshape(-1, 16).T, (8, 1)).astype(np.uint16)


def unstriped(offs):
    return offs[:16].T.reshape(-1).astype(np.int64)


def pack_weight(w):
    k, n = w.shape
    w = f64(np.asarray(w, np.float32).astype(ml_dtypes.bfloat16)).reshape(k // 32, 32, n)
    amax = np.abs(w).max(1)
    byte = np.clip(np.where(amax > 0, np.frexp(amax)[1] - 1 + 127 - 7, 1), 1, 254)
    scaled = (w * np.exp2(127.0 - byte)[:, None, :]).reshape(k, n).astype(np.float32)
    words = np.ascontiguousarray(scaled.reshape(k // 512, 128, 4, n).transpose(0, 1, 3, 2)).astype(ml_dtypes.float8_e4m3fn).view(np.uint8)
    return words, np.ascontiguousarray(byte.astype(np.uint8).reshape(k // 512, 16, n))


def unpack_weight(words, scales):
    g, p, n, _ = words.shape
    vals = np.ascontiguousarray(words).view(ml_dtypes.float8_e4m3fn).astype(np.float64) * np.repeat(np.exp2(scales.astype(np.float64) - 127.0), 8, axis=1)[..., None]
    return vals.transpose(0, 1, 3, 2).reshape(g * 512, n)


def relu(v):
    return np.maximum(v, 0.0)


K, T, S, N = 512, 2048, 1024, 128
P = 2 ** 7


def setup_inputs():
    n = np.random.standard_normal
    s = mx_kscale(K)[:, None]
    packed_w1 = pack_weight(n((K, N)) / np.sqrt(K) / s)
    return {
        "xT": (n((K, T)) * s).astype(np.float32),
        "gate": np.tile(np.random.uniform(0.2, 1.0, S), (P, 1)).astype(np.float32),
        "res": n((N, T)).astype(np.float32),
        "w1_words": packed_w1[0],
        "w1_scales": packed_w1[1],
        "offs": striped(np.random.permutation(T)[:S]),
    }


def reference(xT, gate, res, w1_words, w1_scales, offs):
    r = f64(res)[:, unstriped(offs)]
    xq = mxq(f64(xT)[:, unstriped(offs)], 0, "e4m3")
    y = relu(unpack_weight(w1_words, w1_scales).T @ xq)
    out = f64(res).copy()
    out[:, unstriped(offs)] = r + y * f64(gate)[:1]
    return out

@@ -1,0 +1,108 @@
+from contextlib import ExitStack
+
+import concourse.mybir as mybir
+
+K, T, S, N = 512, 2048, 1024, 128
+FLOPS = 2 * K * S * N
+
+F32 = mybir.dt.float32
+BF16 = mybir.dt.bfloat16
+U32 = mybir.dt.uint32
+I32 = mybir.dt.int32
+U16 = mybir.dt.uint16
+U8 = mybir.dt.uint8
+FP8X4 = mybir.dt.float8_e4m3fn_x4
+ALU = mybir.AluOpType
+
+P = 128
+PIECE = 256
+BANK = 512
+LOADS_LOW = [(0, 1024, 512), (1024, 2048, 640)]
+LOADS_HIGH = [(0, 512, 0), (512, 1024, 0), (1024, 1536, 512), (1536, 2048, 352)]
+
+
+def tile_picked_modres_linrelu_l_kernel(
+    tc, xT, gate, res, w1_words, w1_scales, offs, out
+):
+    nc = tc.nc
+    with ExitStack() as ctx:
+        keep = ctx.enter_context(tc.tile_pool(name="keep", bufs=1))
+        psum = ctx.enter_context(tc.psum_pool(name="psum", bufs=1))
+
+        offsets = keep.tile([P, S // 16], U16, name="offsets")
+        nc.sync.dma_start(offsets[:], offs)
+
+        w_scales = keep.tile([P, N], U8, name="w_scales", align_bytes=64)
+        nc.gpsimd.memset(w_scales[:].bitcast(I32), 0)
+
+        rows = xT.rearrange("(p j) t -> p j t", j=4)
+        pieces = S // PIECE
+        picked = [keep.tile([P, 2, PIECE], U32, name=f"picked{c}") for c in range(pieces)]
+
+        for u, loads in enumerate((LOADS_LOW, LOADS_HIGH)):
+            pairs = keep.tile([P, T, 2], BF16, name=f"pairs{u}")
+            for a, b, by_vector in loads:
+                raw = keep.tile([P, 2, b - a], F32, name=f"raw{u}_{a}")
+                nc.sync.dma_start(raw[:], rows[:, 2 * u : 2 * u + 2, a:b])
+                woven = raw[:].rearrange("p j t -> p t j")
+                if by_vector > 0:
+                    nc.vector.tensor_copy(pairs[:, a : a + by_vector, :], woven[:, :by_vector, :])
+                if by_vector < b - a:
+                    nc.scalar.copy(pairs[:, a + by_vector : b, :], woven[:, by_vector:, :])
+            words = pairs[:].rearrange("p t j -> p (t j)").bitcast(U32)
+            for c in range(pieces):
+                entries = offsets[:, c * PIECE // 16 : (c + 1) * PIECE // 16]
+                nc.vector.tensor_copy(picked[c][:, u, :], words.indirect(entries))
+
+        w_codes = keep.tile([P, N], U32, name="w_codes", align_bytes=64)
+        nc.sync.dma_start(
+            w_codes[:].bitcast(I32), w1_words[0].rearrange("p n t -> p (n t)").bitcast(I32)
+        )
+        for q in range(4):
+            nc.sync.dma_start(
+                w_scales[32 * q : 32 * q + 4, :].bitcast(I32),
+                w1_scales[0, 4 * q : 4 * q + 4, :].bitcast(I32),
+            )
+        stream = keep.tile([P, T], F32, name="stream")
+        nc.sync.dma_start(stream[:], res)
+        gates = keep.tile([P, S], F32, name="gates")
+        nc.sync.dma_start(gates[:], gate)
+
+        update = keep.tile([P, S], F32, name="update")
+        banks = []
+        for h in range(S // BANK):
+            codes = keep.tile([P, BANK], U32, name=f"codes{h}", align_bytes=64)
+            scales = keep.tile([P, BANK], U8, name=f"scales{h}", align_bytes=64)
+            for i in range(BANK // PIECE):
+                c = h * (BANK // PIECE) + i
+                grouped = keep.tile([P, PIECE * 4], BF16, name=f"grouped{c}", tag=f"staged{c}", align_bytes=64)
+                nc.scalar.copy(
+                    grouped[:].bitcast(U32).rearrange("p (n u) -> p n u", u=2),
+                    picked[c][:].rearrange("p u n -> p n u"),
+                )
+                cols = slice(i * PIECE, (i + 1) * PIECE)
+                nc.vector.quantize_mx(
+                    out=codes[:, cols].bitcast(FP8X4), scales=scales[:, cols], in_=grouped[:]
+                )
+            acc = psum.tile([P, BANK], F32, name=f"acc{h}")
+            nc.tensor.matmul_mx(
+                out=acc[:],
+                lhsT=w_codes[:].bitcast(FP8X4),
+                lhsT_scale=w_scales[:],
+                rhs=codes[:].bitcast(FP8X4),
+                rhs_scale=scales[:],
+                start=True,
+                stop=True,
+            )
+            banks.append(acc)
+
+        old = keep.tile([P, S], F32, name="old", tag=f"staged{pieces - 1}", align_bytes=64)
+        nc.vector.tensor_copy(old[:], stream[:].indirect(offsets[:]))
+        for h, acc in enumerate(banks):
+            cols = slice(h * BANK, (h + 1) * BANK)
+            nc.vector.scalar_tensor_tensor(
+                update[:, cols], acc[:], 0.0, gates[:, cols], ALU.max, ALU.mult
+            )
+        nc.vector.tensor_tensor(stream[:].indirect(offsets[:]), old[:], update[:], ALU.add)
+        nc.sync.dma_start(out[:, : T // 2], stream[:, : T // 2])
+        nc.scalar.dma_start(out[:, T // 2 :], stream[:, T // 2 :])

@@ -1,6 +1,7 @@
 from contextlib import ExitStack
 
 import concourse.mybir as mybir
+from concourse.masks import make_identity
 
 K, T, S, N = 512, 2048, 1024, 128
 FLOPS = 2 * K * S * N
@@ -13,12 +14,13 @@ U16 = mybir.dt.uint16
 U8 = mybir.dt.uint8
 FP8X4 = mybir.dt.float8_e4m3fn_x4
 ALU = mybir.AluOpType
+ACT = mybir.ActivationFunctionType
 
 P = 128
 PIECE = 256
-BANK = 512
+SCATTERS = [(0, 512), (512, 1024)]
 LOADS_LOW = [(0, 1024, 512), (1024, 2048, 640)]
-LOADS_HIGH = [(0, 512, 0), (512, 1024, 0), (1024, 1536, 512), (1536, 2048, 352)]
+LOADS_HIGH = [(0, 1024, 256), (1024, 1792, 512), (1792, 2048, 176)]
 
 
 def tile_picked_modres_linrelu_l_kernel(
@@ -29,15 +31,20 @@ def tile_picked_modres_linrelu_l_kernel(
         keep = ctx.enter_context(tc.tile_pool(name="keep", bufs=1))
         psum = ctx.enter_context(tc.psum_pool(name="psum", bufs=1))
 
+        gate_rows = keep.tile([P, P], F32, name="gate_rows")
+        nc.vector.memset(gate_rows[:], 0.0)
+        w_scales = keep.tile([P, N], U8, name="w_scales", align_bytes=64)
+        nc.vector.memset(w_scales[:].bitcast(I32), 0)
+        identity = keep.tile([P, P], F32, name="identity")
+        make_identity(nc, identity[:])
+
         offsets = keep.tile([P, S // 16], U16, name="offsets")
         nc.sync.dma_start(offsets[:], offs)
 
-        w_scales = keep.tile([P, N], U8, name="w_scales", align_bytes=64)
-        nc.gpsimd.memset(w_scales[:].bitcast(I32), 0)
-
         rows = xT.rearrange("(p j) t -> p j t", j=4)
         pieces = S // PIECE
-        picked = [keep.tile([P, 2, PIECE], U32, name=f"picked{c}") for c in range(pieces)]
+        blocks = PIECE // P
+        picked = [keep.tile([P, 2, PIECE], U32, name=f"picked{c}", tag=f"picked{c}") for c in range(pieces)]
 
         for u, loads in enumerate((LOADS_LOW, LOADS_HIGH)):
             pairs = keep.tile([P, T, 2], BF16, name=f"pairs{u}")
@@ -45,15 +52,20 @@ def tile_picked_modres_linrelu_l_kernel(
                 raw = keep.tile([P, 2, b - a], F32, name=f"raw{u}_{a}")
                 nc.sync.dma_start(raw[:], rows[:, 2 * u : 2 * u + 2, a:b])
                 woven = raw[:].rearrange("p j t -> p t j")
-                if by_vector > 0:
-                    nc.vector.tensor_copy(pairs[:, a : a + by_vector, :], woven[:, :by_vector, :])
-                if by_vector < b - a:
-                    nc.scalar.copy(pairs[:, a + by_vector : b, :], woven[:, by_vector:, :])
+                nc.vector.tensor_copy(pairs[:, a : a + by_vector, :], woven[:, :by_vector, :])
+                nc.scalar.copy(pairs[:, a + by_vector : b, :], woven[:, by_vector:, :])
             words = pairs[:].rearrange("p t j -> p (t j)").bitcast(U32)
             for c in range(pieces):
                 entries = offsets[:, c * PIECE // 16 : (c + 1) * PIECE // 16]
                 nc.vector.tensor_copy(picked[c][:, u, :], words.indirect(entries))
 
+        stream = keep.tile([P, T], F32, name="stream")
+        nc.sync.dma_start(stream[:], res)
+        nc.sync.dma_start(gate_rows[: S // P, :], gate[0].rearrange("(b p) -> b p", p=P))
+        gate_turned = psum.tile([P, P], F32, name="gate_turned")
+        nc.tensor.transpose(gate_turned[:], gate_rows[:], identity[:])
+        gate_cols = keep.tile([P, S // P], F32, name="gate_cols")
+        nc.scalar.copy(gate_cols[:], gate_turned[:, : S // P])
         w_codes = keep.tile([P, N], U32, name="w_codes", align_bytes=64)
         nc.sync.dma_start(
             w_codes[:].bitcast(I32), w1_words[0].rearrange("p n t -> p (n t)").bitcast(I32)
@@ -63,46 +75,60 @@ def tile_picked_modres_linrelu_l_kernel(
                 w_scales[32 * q : 32 * q + 4, :].bitcast(I32),
                 w1_scales[0, 4 * q : 4 * q + 4, :].bitcast(I32),
             )
-        stream = keep.tile([P, T], F32, name="stream")
-        nc.sync.dma_start(stream[:], res)
-        gates = keep.tile([P, S], F32, name="gates")
-        nc.sync.dma_start(gates[:], gate)
 
-        update = keep.tile([P, S], F32, name="update")
-        banks = []
-        for h in range(S // BANK):
-            codes = keep.tile([P, BANK], U32, name=f"codes{h}", align_bytes=64)
-            scales = keep.tile([P, BANK], U8, name=f"scales{h}", align_bytes=64)
-            for i in range(BANK // PIECE):
-                c = h * (BANK // PIECE) + i
-                grouped = keep.tile([P, PIECE * 4], BF16, name=f"grouped{c}", tag=f"staged{c}", align_bytes=64)
-                nc.scalar.copy(
-                    grouped[:].bitcast(U32).rearrange("p (n u) -> p n u", u=2),
-                    picked[c][:].rearrange("p u n -> p n u"),
-                )
-                cols = slice(i * PIECE, (i + 1) * PIECE)
-                nc.vector.quantize_mx(
-                    out=codes[:, cols].bitcast(FP8X4), scales=scales[:, cols], in_=grouped[:]
-                )
-            acc = psum.tile([P, BANK], F32, name=f"acc{h}")
-            nc.tensor.matmul_mx(
-                out=acc[:],
-                lhsT=w_codes[:].bitcast(FP8X4),
-                lhsT_scale=w_scales[:],
-                rhs=codes[:].bitcast(FP8X4),
-                rhs_scale=scales[:],
-                start=True,
-                stop=True,
+        grouped = []
+        for c in range(pieces):
+            tile = keep.tile([P, PIECE * 4], BF16, name=f"grouped{c}", align_bytes=64)
+            nc.scalar.copy(
+                tile[:].bitcast(U32).rearrange("p (n u) -> p n u", u=2),
+                picked[c][:].rearrange("p u n -> p n u"),
             )
-            banks.append(acc)
+            grouped.append(tile)
 
-        old = keep.tile([P, S], F32, name="old", tag=f"staged{pieces - 1}", align_bytes=64)
+        quantised = []
+        for c in range(pieces):
+            codes = keep.tile([P, PIECE], U32, name=f"codes{c}", align_bytes=64)
+            scales = keep.tile([P, PIECE], U8, name=f"scales{c}", align_bytes=64)
+            nc.vector.quantize_mx(
+                out=codes[:].bitcast(FP8X4), scales=scales[:], in_=grouped[c][:]
+            )
+            quantised.append((codes, scales))
+
+        updates = [keep.tile([P, b - a], F32, name=f"update{a}") for a, b in SCATTERS]
+        for c, (codes, scales) in enumerate(quantised):
+            acc = psum.tile([P, blocks, N], F32, name=f"acc{c}", tag=f"bank{(2 * c + c // 2) % 4}")
+            for i in range(blocks):
+                cols = slice(i * P, (i + 1) * P)
+                nc.tensor.matmul_mx(
+                    out=acc[:, i, :],
+                    lhsT=codes[:, cols].bitcast(FP8X4),
+                    lhsT_scale=scales[:, cols],
+                    rhs=w_codes[:].bitcast(FP8X4),
+                    rhs_scale=w_scales[:],
+                    start=True,
+                    stop=True,
+                )
+            active = keep.tile([P, blocks, N], F32, name=f"active{c}")
+            nc.scalar.activation(active[:], acc[:], ACT.Relu)
+            gated = keep.tile([P, blocks, N], F32, name=f"gated{c}")
+            back = psum.tile([P, blocks, P], F32, name=f"back{c}", tag=f"bank{(2 * c + 1 - c // 2) % 4}")
+            for i in range(blocks):
+                b = c * blocks + i
+                nc.scalar.activation(
+                    gated[:, i, :], active[:, i, :], ACT.Copy, scale=gate_cols[:, b : b + 1]
+                )
+                nc.tensor.transpose(back[:, i, :], gated[:, i, :], identity[:])
+            s = max(j for j, (a, b) in enumerate(SCATTERS) if a <= c * PIECE)
+            first = c * PIECE - SCATTERS[s][0]
+            nc.scalar.copy(
+                updates[s][:, first : first + PIECE], back[:].rearrange("p i n -> p (i n)")
+            )
+
+        old = keep.tile([P, S], F32, name="old", tag=f"picked{pieces - 2}")
         nc.vector.tensor_copy(old[:], stream[:].indirect(offsets[:]))
-        for h, acc in enumerate(banks):
-            cols = slice(h * BANK, (h + 1) * BANK)
-            nc.vector.scalar_tensor_tensor(
-                update[:, cols], acc[:], 0.0, gates[:, cols], ALU.max, ALU.mult
+        for (a, b), update in zip(SCATTERS, updates):
+            nc.vector.tensor_tensor(
+                stream[:].indirect(offsets[:, a // 16 : b // 16]), old[:, a:b], update[:], ALU.add
             )
-        nc.vector.tensor_tensor(stream[:].indirect(offsets[:]), old[:], update[:], ALU.add)
         nc.sync.dma_start(out[:, : T // 2], stream[:, : T // 2])
         nc.scalar.dma_start(out[:, T // 2 :], stream[:, T // 2 :])

@@ -19,8 +19,8 @@ ACT = mybir.ActivationFunctionType
 P = 128
 PIECE = 256
 SCATTERS = [(0, 512), (512, 1024)]
-LOADS_LOW = [(0, 1024, 512), (1024, 2048, 640)]
-LOADS_HIGH = [(0, 1024, 256), (1024, 1792, 512), (1792, 2048, 176)]
+LOADS_LOW = [(0, 1280, 640), (1280, 2048, 448)]
+LOADS_HIGH = [(0, 1024, 256), (1024, 1792, 448), (1792, 2048, 128)]
 
 
 def tile_picked_modres_linrelu_l_kernel(
@@ -39,7 +39,6 @@ def tile_picked_modres_linrelu_l_kernel(
         make_identity(nc, identity[:])
 
         offsets = keep.tile([P, S // 16], U16, name="offsets")
-        nc.sync.dma_start(offsets[:], offs)
 
         rows = xT.rearrange("(p j) t -> p j t", j=4)
         pieces = S // PIECE
@@ -49,8 +48,10 @@ def tile_picked_modres_linrelu_l_kernel(
         for u, loads in enumerate((LOADS_LOW, LOADS_HIGH)):
             pairs = keep.tile([P, T, 2], BF16, name=f"pairs{u}")
             for a, b, by_vector in loads:
-                raw = keep.tile([P, 2, b - a], F32, name=f"raw{u}_{a}")
+                raw = keep.tile([P, 2, b - a], F32, name=f"raw{u}_{a}", align_bytes=256)
                 nc.sync.dma_start(raw[:], rows[:, 2 * u : 2 * u + 2, a:b])
+                if (u, a) == (0, 0):
+                    nc.sync.dma_start(offsets[:], offs)
                 woven = raw[:].rearrange("p j t -> p t j")
                 nc.vector.tensor_copy(pairs[:, a : a + by_vector, :], woven[:, :by_vector, :])
                 nc.scalar.copy(pairs[:, a + by_vector : b, :], woven[:, by_vector:, :])
@@ -59,7 +60,7 @@ def tile_picked_modres_linrelu_l_kernel(
                 entries = offsets[:, c * PIECE // 16 : (c + 1) * PIECE // 16]
                 nc.vector.tensor_copy(picked[c][:, u, :], words.indirect(entries))
 
-        stream = keep.tile([P, T], F32, name="stream")
+        stream = keep.tile([P, T], F32, name="stream", align_bytes=256)
         nc.sync.dma_start(stream[:], res)
         nc.sync.dma_start(gate_rows[: S // P, :], gate[0].rearrange("(b p) -> b p", p=P))
         gate_turned = psum.tile([P, P], F32, name="gate_turned")

@@ -19,8 +19,6 @@ ACT = mybir.ActivationFunctionType
 P = 128
 PIECE = 256
 SCATTERS = [(0, 512), (512, 1024)]
-LOADS_LOW = [(0, 1280, 640), (1280, 2048, 448)]
-LOADS_HIGH = [(0, 1024, 256), (1024, 1792, 448), (1792, 2048, 128)]
 
 
 def tile_picked_modres_linrelu_l_kernel(
@@ -43,22 +41,21 @@ def tile_picked_modres_linrelu_l_kernel(
         rows = xT.rearrange("(p j) t -> p j t", j=4)
         pieces = S // PIECE
         blocks = PIECE // P
-        picked = [keep.tile([P, 2, PIECE], U32, name=f"picked{c}", tag=f"picked{c}") for c in range(pieces)]
+        picked = keep.tile([P, pieces, 2, PIECE], U32, name="picked", tag="picked")
+        halves = picked[:].bitcast(BF16).rearrange("p c u (n e) -> p c u n e", e=2)
 
-        for u, loads in enumerate((LOADS_LOW, LOADS_HIGH)):
-            pairs = keep.tile([P, T, 2], BF16, name=f"pairs{u}")
-            for a, b, by_vector in loads:
-                raw = keep.tile([P, 2, b - a], F32, name=f"raw{u}_{a}", align_bytes=256)
-                nc.sync.dma_start(raw[:], rows[:, 2 * u : 2 * u + 2, a:b])
-                if (u, a) == (0, 0):
-                    nc.sync.dma_start(offsets[:], offs)
-                woven = raw[:].rearrange("p j t -> p t j")
-                nc.vector.tensor_copy(pairs[:, a : a + by_vector, :], woven[:, :by_vector, :])
-                nc.scalar.copy(pairs[:, a + by_vector : b, :], woven[:, by_vector:, :])
-            words = pairs[:].rearrange("p t j -> p (t j)").bitcast(U32)
-            for c in range(pieces):
-                entries = offsets[:, c * PIECE // 16 : (c + 1) * PIECE // 16]
-                nc.vector.tensor_copy(picked[c][:, u, :], words.indirect(entries))
+        for j in range(3):
+            plane = keep.tile([P, T], F32, name=f"plane{j}", align_bytes=256)
+            nc.sync.dma_start(plane[:], rows[:, j, :])
+            if j == 0:
+                nc.sync.dma_start(offsets[:], offs)
+            nc.vector.tensor_copy(halves[:, :, j // 2, :, j % 2], plane[:].indirect(offsets[:]))
+
+        late = keep.tile([P, T], F32, name="late", align_bytes=256)
+        nc.sync.dma_start(late[:], rows[:, 3, :])
+        for c in range(pieces):
+            entries = offsets[:, c * PIECE // 16 : (c + 1) * PIECE // 16]
+            nc.vector.tensor_copy(halves[:, c, 1, :, 1], late[:].indirect(entries))
 
         stream = keep.tile([P, T], F32, name="stream", align_bytes=256)
         nc.sync.dma_start(stream[:], res)
@@ -79,10 +76,10 @@ def tile_picked_modres_linrelu_l_kernel(
 
         grouped = []
         for c in range(pieces):
-            tile = keep.tile([P, PIECE * 4], BF16, name=f"grouped{c}", align_bytes=64)
+            tile = keep.tile([P, PIECE * 4], BF16, name=f"grouped{c}", tag=f"grouped{c}", align_bytes=64)
             nc.scalar.copy(
                 tile[:].bitcast(U32).rearrange("p (n u) -> p n u", u=2),
-                picked[c][:].rearrange("p u n -> p n u"),
+                picked[:, c, :, :].rearrange("p u n -> p n u"),
             )
             grouped.append(tile)
 
@@ -125,7 +122,7 @@ def tile_picked_modres_linrelu_l_kernel(
                 updates[s][:, first : first + PIECE], back[:].rearrange("p i n -> p (i n)")
             )
 
-        old = keep.tile([P, S], F32, name="old", tag=f"picked{pieces - 2}")
+        old = keep.tile([P, S], F32, name="old", tag=f"grouped{pieces - 3}", align_bytes=64)
         nc.vector.tensor_copy(old[:], stream[:].indirect(offsets[:]))
         for (a, b), update in zip(SCATTERS, updates):
             nc.vector.tensor_tensor(

@@ -44,26 +44,35 @@ def tile_picked_modres_linrelu_l_kernel(
         picked = keep.tile([P, pieces, 2, PIECE], U32, name="picked", tag="picked")
         halves = picked[:].bitcast(BF16).rearrange("p c u (n e) -> p c u n e", e=2)
 
-        for j in range(3):
+        shared = pieces - 1
+        own = offsets[:, : shared * PIECE // 16]
+        lent = offsets[:, shared * PIECE // 16 :]
+        for j in (0, 2, 1):
             plane = keep.tile([P, T], F32, name=f"plane{j}", align_bytes=256)
             nc.sync.dma_start(plane[:], rows[:, j, :])
             if j == 0:
                 nc.sync.dma_start(offsets[:], offs)
-            nc.vector.tensor_copy(halves[:, :, j // 2, :, j % 2], plane[:].indirect(offsets[:]))
+            if j == 2:
+                nc.vector.tensor_copy(halves[:, :shared, 1, :, 0], plane[:].indirect(own))
+                rounded = keep.tile([P, T], BF16, name="rounded2")
+                nc.scalar.copy(rounded[:], plane[:])
+                nc.scalar.activation(halves[:, shared, 1, :, 0], rounded[:].indirect(lent), ACT.Copy)
+            else:
+                nc.vector.tensor_copy(halves[:, :, 0, :, j], plane[:].indirect(offsets[:]))
 
         late = keep.tile([P, T], F32, name="late", align_bytes=256)
-        nc.sync.dma_start(late[:], rows[:, 3, :])
-        for c in range(pieces):
+        rounded = keep.tile([P, T], BF16, name="rounded3")
+        nc.sync.dma_start(late[:, : T // 2], rows[:, 3, : T // 2])
+        nc.sync.dma_start(late[:, T // 2 :], rows[:, 3, T // 2 :])
+        nc.scalar.copy(rounded[:, : T // 2], late[:, : T // 2])
+        nc.scalar.copy(rounded[:, T // 2 : 3 * T // 4], late[:, T // 2 : 3 * T // 4])
+        nc.gpsimd.tensor_copy(rounded[:, 3 * T // 4 :], late[:, 3 * T // 4 :])
+        for c in range(shared):
             entries = offsets[:, c * PIECE // 16 : (c + 1) * PIECE // 16]
             nc.vector.tensor_copy(halves[:, c, 1, :, 1], late[:].indirect(entries))
 
         stream = keep.tile([P, T], F32, name="stream", align_bytes=256)
         nc.sync.dma_start(stream[:], res)
-        nc.sync.dma_start(gate_rows[: S // P, :], gate[0].rearrange("(b p) -> b p", p=P))
-        gate_turned = psum.tile([P, P], F32, name="gate_turned")
-        nc.tensor.transpose(gate_turned[:], gate_rows[:], identity[:])
-        gate_cols = keep.tile([P, S // P], F32, name="gate_cols")
-        nc.scalar.copy(gate_cols[:], gate_turned[:, : S // P])
         w_codes = keep.tile([P, N], U32, name="w_codes", align_bytes=64)
         nc.sync.dma_start(
             w_codes[:].bitcast(I32), w1_words[0].rearrange("p n t -> p (n t)").bitcast(I32)
@@ -73,24 +82,36 @@ def tile_picked_modres_linrelu_l_kernel(
                 w_scales[32 * q : 32 * q + 4, :].bitcast(I32),
                 w1_scales[0, 4 * q : 4 * q + 4, :].bitcast(I32),
             )
+        nc.sync.dma_start(gate_rows[: S // P, :], gate[0].rearrange("(b p) -> b p", p=P))
+        gate_turned = psum.tile([P, P], F32, name="gate_turned")
+        nc.tensor.transpose(gate_turned[:], gate_rows[:], identity[:])
+        gate_cols = keep.tile([P, S // P], F32, name="gate_cols")
+        nc.scalar.copy(gate_cols[:], gate_turned[:, : S // P])
 
-        grouped = []
-        for c in range(pieces):
-            tile = keep.tile([P, PIECE * 4], BF16, name=f"grouped{c}", tag=f"grouped{c}", align_bytes=64)
-            nc.scalar.copy(
-                tile[:].bitcast(U32).rearrange("p (n u) -> p n u", u=2),
-                picked[:, c, :, :].rearrange("p u n -> p n u"),
-            )
-            grouped.append(tile)
+        def quantise(name, grouped, width):
+            codes = keep.tile([P, width], U32, name=f"codes{name}", align_bytes=64)
+            scales = keep.tile([P, width], U8, name=f"scales{name}", align_bytes=64)
+            nc.vector.quantize_mx(out=codes[:].bitcast(FP8X4), scales=scales[:], in_=grouped[:])
+            return [(codes[:, a : a + PIECE], scales[:, a : a + PIECE]) for a in range(0, width, PIECE)]
 
         quantised = []
-        for c in range(pieces):
-            codes = keep.tile([P, PIECE], U32, name=f"codes{c}", align_bytes=64)
-            scales = keep.tile([P, PIECE], U8, name=f"scales{c}", align_bytes=64)
-            nc.vector.quantize_mx(
-                out=codes[:].bitcast(FP8X4), scales=scales[:], in_=grouped[c][:]
+        for c in range(2):
+            grouped = keep.tile([P, PIECE * 4], BF16, name=f"grouped{c}", tag=f"grouped{c}", align_bytes=64)
+            nc.scalar.copy(
+                grouped[:].bitcast(U32).rearrange("p (n u) -> p n u", u=2),
+                picked[:, c, :, :].rearrange("p u n -> p n u"),
             )
-            quantised.append((codes, scales))
+            quantised.extend(quantise(c, grouped, PIECE))
+        nc.scalar.activation(halves[:, shared, 1, :, 1], rounded[:].indirect(lent), ACT.Copy)
+        old = keep.tile([P, S], F32, name="old", tag="grouped0", align_bytes=64)
+        nc.vector.tensor_copy(old[:], stream[:].indirect(offsets[:]))
+        grouped = keep.tile([P, 2 * PIECE * 4], BF16, name="grouped2", tag="grouped1", align_bytes=64)
+        for c in (2, 3):
+            nc.gpsimd.tensor_copy(
+                grouped[:, (c - 2) * PIECE * 4 : (c - 1) * PIECE * 4].bitcast(U32).rearrange("p (n u) -> p n u", u=2),
+                picked[:, c, :, :].rearrange("p u n -> p n u"),
+            )
+        quantised.extend(quantise(2, grouped, 2 * PIECE))
 
         updates = [keep.tile([P, b - a], F32, name=f"update{a}") for a, b in SCATTERS]
         for c, (codes, scales) in enumerate(quantised):
@@ -122,8 +143,6 @@ def tile_picked_modres_linrelu_l_kernel(
                 updates[s][:, first : first + PIECE], back[:].rearrange("p i n -> p (i n)")
             )
 
-        old = keep.tile([P, S], F32, name="old", tag=f"grouped{pieces - 3}", align_bytes=64)
-        nc.vector.tensor_copy(old[:], stream[:].indirect(offsets[:]))
         for (a, b), update in zip(SCATTERS, updates):
             nc.vector.tensor_tensor(
                 stream[:].indirect(offsets[:, a // 16 : b // 16]), old[:, a:b], update[:], ALU.add

@@ -73,6 +73,11 @@ def tile_picked_modres_linrelu_l_kernel(
 
         stream = keep.tile([P, T], F32, name="stream", align_bytes=256)
         nc.sync.dma_start(stream[:], res)
+        nc.sync.dma_start(gate_rows[: S // P, :], gate[0].rearrange("(b p) -> b p", p=P))
+        gate_turned = psum.tile([P, P], F32, name="gate_turned")
+        nc.tensor.transpose(gate_turned[:], gate_rows[:], identity[:])
+        gate_cols = keep.tile([P, S // P], F32, name="gate_cols")
+        nc.scalar.copy(gate_cols[:], gate_turned[:, : S // P])
         w_codes = keep.tile([P, N], U32, name="w_codes", align_bytes=64)
         nc.sync.dma_start(
             w_codes[:].bitcast(I32), w1_words[0].rearrange("p n t -> p (n t)").bitcast(I32)
@@ -82,11 +87,6 @@ def tile_picked_modres_linrelu_l_kernel(
                 w_scales[32 * q : 32 * q + 4, :].bitcast(I32),
                 w1_scales[0, 4 * q : 4 * q + 4, :].bitcast(I32),
             )
-        nc.sync.dma_start(gate_rows[: S // P, :], gate[0].rearrange("(b p) -> b p", p=P))
-        gate_turned = psum.tile([P, P], F32, name="gate_turned")
-        nc.tensor.transpose(gate_turned[:], gate_rows[:], identity[:])
-        gate_cols = keep.tile([P, S // P], F32, name="gate_cols")
-        nc.scalar.copy(gate_cols[:], gate_turned[:, : S // P])
 
         def quantise(name, grouped, width):
             codes = keep.tile([P, width], U32, name=f"codes{name}", align_bytes=64)
@@ -147,5 +147,4 @@ def tile_picked_modres_linrelu_l_kernel(
             nc.vector.tensor_tensor(
                 stream[:].indirect(offsets[:, a // 16 : b // 16]), old[:, a:b], update[:], ALU.add
             )
-        nc.sync.dma_start(out[:, : T // 2], stream[:, : T // 2])
-        nc.scalar.dma_start(out[:, T // 2 :], stream[:, T // 2 :])
+        nc.sync.dma_start(out, stream[:])

@@ -62,11 +62,9 @@ def tile_picked_modres_linrelu_l_kernel(
 
         late = keep.tile([P, T], F32, name="late", align_bytes=256)
         rounded = keep.tile([P, T], BF16, name="rounded3")
-        nc.sync.dma_start(late[:, : T // 2], rows[:, 3, : T // 2])
-        nc.sync.dma_start(late[:, T // 2 :], rows[:, 3, T // 2 :])
+        nc.sync.dma_start(late[:], rows[:, 3, :])
         nc.scalar.copy(rounded[:, : T // 2], late[:, : T // 2])
-        nc.scalar.copy(rounded[:, T // 2 : 3 * T // 4], late[:, T // 2 : 3 * T // 4])
-        nc.gpsimd.tensor_copy(rounded[:, 3 * T // 4 :], late[:, 3 * T // 4 :])
+        nc.gpsimd.tensor_copy(rounded[:, T // 2 :], late[:, T // 2 :])
         for c in range(shared):
             entries = offsets[:, c * PIECE // 16 : (c + 1) * PIECE // 16]
             nc.vector.tensor_copy(halves[:, c, 1, :, 1], late[:].indirect(entries))

@@ -63,8 +63,8 @@ def tile_picked_modres_linrelu_l_kernel(
         late = keep.tile([P, T], F32, name="late", align_bytes=256)
         rounded = keep.tile([P, T], BF16, name="rounded3")
         nc.sync.dma_start(late[:], rows[:, 3, :])
-        nc.scalar.copy(rounded[:, : T // 2], late[:, : T // 2])
-        nc.gpsimd.tensor_copy(rounded[:, T // 2 :], late[:, T // 2 :])
+        nc.scalar.copy(rounded[:, :768], late[:, :768])
+        nc.gpsimd.tensor_copy(rounded[:, 768:], late[:, 768:])
         for c in range(shared):
             entries = offsets[:, c * PIECE // 16 : (c + 1) * PIECE // 16]
             nc.vector.tensor_copy(halves[:, c, 1, :, 1], late[:].indirect(entries))

@@ -36,6 +36,12 @@ def tile_picked_modres_linrelu_l_kernel(
         identity = keep.tile([P, P], F32, name="identity")
         make_identity(nc, identity[:])
 
+        for q in range(4):
+            nc.scalar.dma_start(
+                w_scales[32 * q : 32 * q + 4, :].bitcast(I32),
+                w1_scales[0, 4 * q : 4 * q + 4, :].bitcast(I32),
+            )
+
         offsets = keep.tile([P, S // 16], U16, name="offsets")
 
         rows = xT.rearrange("(p j) t -> p j t", j=4)
@@ -80,11 +86,6 @@ def tile_picked_modres_linrelu_l_kernel(
         nc.sync.dma_start(
             w_codes[:].bitcast(I32), w1_words[0].rearrange("p n t -> p (n t)").bitcast(I32)
         )
-        for q in range(4):
-            nc.sync.dma_start(
-                w_scales[32 * q : 32 * q + 4, :].bitcast(I32),
-                w1_scales[0, 4 * q : 4 * q + 4, :].bitcast(I32),
-            )
 
         def quantise(name, grouped, width):
             codes = keep.tile([P, width], U32, name=f"codes{name}", align_bytes=64)
@@ -101,8 +102,8 @@ def tile_picked_modres_linrelu_l_kernel(
             )
             quantised.extend(quantise(c, grouped, PIECE))
         nc.scalar.activation(halves[:, shared, 1, :, 1], rounded[:].indirect(lent), ACT.Copy)
-        old = keep.tile([P, S], F32, name="old", tag="grouped0", align_bytes=64)
-        nc.vector.tensor_copy(old[:], stream[:].indirect(offsets[:]))
+        old = picked[:, :2, :, :].rearrange("p c u n -> p (c u n)").bitcast(F32)
+        nc.vector.tensor_copy(old, stream[:].indirect(offsets[:]))
         grouped = keep.tile([P, 2 * PIECE * 4], BF16, name="grouped2", tag="grouped1", align_bytes=64)
         for c in (2, 3):
             nc.gpsimd.tensor_copy(

@@ -41,6 +41,7 @@ def tile_picked_modres_linrelu_l_kernel(
                 w_scales[32 * q : 32 * q + 4, :].bitcast(I32),
                 w1_scales[0, 4 * q : 4 * q + 4, :].bitcast(I32),
             )
+        nc.scalar.dma_start(gate_rows[: S // P, :], gate[0].rearrange("(b p) -> b p", p=P))
 
         offsets = keep.tile([P, S // 16], U16, name="offsets")
 
@@ -50,7 +51,7 @@ def tile_picked_modres_linrelu_l_kernel(
         picked = keep.tile([P, pieces, 2, PIECE], U32, name="picked", tag="picked")
         halves = picked[:].bitcast(BF16).rearrange("p c u (n e) -> p c u n e", e=2)
 
-        shared = pieces - 1
+        shared = pieces - 2
         own = offsets[:, : shared * PIECE // 16]
         lent = offsets[:, shared * PIECE // 16 :]
         for j in (0, 2, 1):
@@ -62,22 +63,21 @@ def tile_picked_modres_linrelu_l_kernel(
                 nc.vector.tensor_copy(halves[:, :shared, 1, :, 0], plane[:].indirect(own))
                 rounded = keep.tile([P, T], BF16, name="rounded2")
                 nc.scalar.copy(rounded[:], plane[:])
-                nc.scalar.activation(halves[:, shared, 1, :, 0], rounded[:].indirect(lent), ACT.Copy)
+                nc.scalar.activation(halves[:, shared:, 1, :, 0], rounded[:].indirect(lent), ACT.Copy)
             else:
                 nc.vector.tensor_copy(halves[:, :, 0, :, j], plane[:].indirect(offsets[:]))
 
         late = keep.tile([P, T], F32, name="late", align_bytes=256)
         rounded = keep.tile([P, T], BF16, name="rounded3")
         nc.sync.dma_start(late[:], rows[:, 3, :])
-        nc.scalar.copy(rounded[:, :768], late[:, :768])
-        nc.gpsimd.tensor_copy(rounded[:, 768:], late[:, 768:])
+        nc.scalar.copy(rounded[:, :576], late[:, :576])
+        nc.gpsimd.tensor_copy(rounded[:, 576:], late[:, 576:])
         for c in range(shared):
             entries = offsets[:, c * PIECE // 16 : (c + 1) * PIECE // 16]
             nc.vector.tensor_copy(halves[:, c, 1, :, 1], late[:].indirect(entries))
 
         stream = keep.tile([P, T], F32, name="stream", align_bytes=256)
         nc.sync.dma_start(stream[:], res)
-        nc.sync.dma_start(gate_rows[: S // P, :], gate[0].rearrange("(b p) -> b p", p=P))
         gate_turned = psum.tile([P, P], F32, name="gate_turned")
         nc.tensor.transpose(gate_turned[:], gate_rows[:], identity[:])
         gate_cols = keep.tile([P, S // P], F32, name="gate_cols")
@@ -101,7 +101,9 @@ def tile_picked_modres_linrelu_l_kernel(
                 picked[:, c, :, :].rearrange("p u n -> p n u"),
             )
             quantised.extend(quantise(c, grouped, PIECE))
-        nc.scalar.activation(halves[:, shared, 1, :, 1], rounded[:].indirect(lent), ACT.Copy)
+        for c in range(shared, pieces):
+            entries = offsets[:, c * PIECE // 16 : (c + 1) * PIECE // 16]
+            nc.scalar.activation(halves[:, c, 1, :, 1], rounded[:].indirect(entries), ACT.Copy)
         old = picked[:, :2, :, :].rearrange("p c u n -> p (c u n)").bitcast(F32)
         nc.vector.tensor_copy(old, stream[:].indirect(offsets[:]))
         grouped = keep.tile([P, 2 * PIECE * 4], BF16, name="grouped2", tag="grouped1", align_bytes=64)

@@ -52,7 +52,12 @@ def tile_picked_modres_linrelu_l_kernel(
         halves = picked[:].bitcast(BF16).rearrange("p c u (n e) -> p c u n e", e=2)
 
         shared = pieces - 2
-        own = offsets[:, : shared * PIECE // 16]
+        direct = keep.tile([P, PIECE * 4], BF16, name="grouped0", tag="grouped0", align_bytes=64)
+        low = keep.tile([P, PIECE], U32, name="low")
+        low_halves = low[:].bitcast(BF16).rearrange("p (n e) -> p n e", e=2)
+        quads = direct[:].rearrange("p (n j) -> p n j", j=4)
+        first = offsets[:, : PIECE // 16]
+        second = offsets[:, PIECE // 16 : 2 * PIECE // 16]
         lent = offsets[:, shared * PIECE // 16 :]
         for j in (0, 2, 1):
             plane = keep.tile([P, T], F32, name=f"plane{j}", align_bytes=256)
@@ -60,21 +65,23 @@ def tile_picked_modres_linrelu_l_kernel(
             if j == 0:
                 nc.sync.dma_start(offsets[:], offs)
             if j == 2:
-                nc.vector.tensor_copy(halves[:, :shared, 1, :, 0], plane[:].indirect(own))
+                nc.vector.tensor_copy(halves[:, 1, 1, :, 0], plane[:].indirect(second))
+                nc.vector.tensor_copy(quads[:, :, 2], plane[:].indirect(first))
                 rounded = keep.tile([P, T], BF16, name="rounded2")
                 nc.scalar.copy(rounded[:], plane[:])
                 nc.scalar.activation(halves[:, shared:, 1, :, 0], rounded[:].indirect(lent), ACT.Copy)
             else:
-                nc.vector.tensor_copy(halves[:, :, 0, :, j], plane[:].indirect(offsets[:]))
+                nc.vector.tensor_copy(low_halves[:, :, j], plane[:].indirect(first))
+                nc.vector.tensor_copy(halves[:, 1:, 0, :, j], plane[:].indirect(offsets[:, PIECE // 16 :]))
+        nc.scalar.copy(direct[:].bitcast(U32).rearrange("p (n u) -> p n u", u=2)[:, :, 0], low[:])
 
         late = keep.tile([P, T], F32, name="late", align_bytes=256)
         rounded = keep.tile([P, T], BF16, name="rounded3")
         nc.sync.dma_start(late[:], rows[:, 3, :])
         nc.scalar.copy(rounded[:, :576], late[:, :576])
         nc.gpsimd.tensor_copy(rounded[:, 576:], late[:, 576:])
-        for c in range(shared):
-            entries = offsets[:, c * PIECE // 16 : (c + 1) * PIECE // 16]
-            nc.vector.tensor_copy(halves[:, c, 1, :, 1], late[:].indirect(entries))
+        nc.vector.tensor_copy(halves[:, 1, 1, :, 1], late[:].indirect(second))
+        nc.vector.tensor_copy(quads[:, :, 3], late[:].indirect(first))
 
         stream = keep.tile([P, T], F32, name="stream", align_bytes=256)
         nc.sync.dma_start(stream[:], res)
@@ -93,14 +100,12 @@ def tile_picked_modres_linrelu_l_kernel(
             nc.vector.quantize_mx(out=codes[:].bitcast(FP8X4), scales=scales[:], in_=grouped[:])
             return [(codes[:, a : a + PIECE], scales[:, a : a + PIECE]) for a in range(0, width, PIECE)]
 
-        quantised = []
-        for c in range(2):
-            grouped = keep.tile([P, PIECE * 4], BF16, name=f"grouped{c}", tag=f"grouped{c}", align_bytes=64)
-            nc.scalar.copy(
-                grouped[:].bitcast(U32).rearrange("p (n u) -> p n u", u=2),
-                picked[:, c, :, :].rearrange("p u n -> p n u"),
-            )
-            quantised.extend(quantise(c, grouped, PIECE))
+        grouped = keep.tile([P, PIECE * 4], BF16, name="grouped1", tag="grouped1", align_bytes=64)
+        nc.scalar.copy(
+            grouped[:].bitcast(U32).rearrange("p (n u) -> p n u", u=2),
+            picked[:, 1, :, :].rearrange("p u n -> p n u"),
+        )
+        quantised = quantise(0, direct, PIECE) + quantise(1, grouped, PIECE)
         for c in range(shared, pieces):
             entries = offsets[:, c * PIECE // 16 : (c + 1) * PIECE // 16]
             nc.scalar.activation(halves[:, c, 1, :, 1], rounded[:].indirect(entries), ACT.Copy)
@@ -115,8 +120,8 @@ def tile_picked_modres_linrelu_l_kernel(
         quantised.extend(quantise(2, grouped, 2 * PIECE))
 
         updates = [keep.tile([P, b - a], F32, name=f"update{a}") for a, b in SCATTERS]
-        for c, (codes, scales) in enumerate(quantised):
-            acc = psum.tile([P, blocks, N], F32, name=f"acc{c}", tag=f"bank{(2 * c + c // 2) % 4}")
+        for turn, (c, (codes, scales)) in enumerate(zip((0, 1, 2, 3), quantised)):
+            acc = psum.tile([P, blocks, N], F32, name=f"acc{c}", tag=f"bank{(2 * turn + turn // 2) % 4}")
             for i in range(blocks):
                 cols = slice(i * P, (i + 1) * P)
                 nc.tensor.matmul_mx(
@@ -131,7 +136,7 @@ def tile_picked_modres_linrelu_l_kernel(
             active = keep.tile([P, blocks, N], F32, name=f"active{c}")
             nc.scalar.activation(active[:], acc[:], ACT.Relu)
             gated = keep.tile([P, blocks, N], F32, name=f"gated{c}")
-            back = psum.tile([P, blocks, P], F32, name=f"back{c}", tag=f"bank{(2 * c + 1 - c // 2) % 4}")
+            back = psum.tile([P, blocks, P], F32, name=f"back{c}", tag=f"bank{(2 * turn + 1 - turn // 2) % 4}")
             for i in range(blocks):
                 b = c * blocks + i
                 nc.scalar.activation(
@@ -139,9 +144,9 @@ def tile_picked_modres_linrelu_l_kernel(
                 )
                 nc.tensor.transpose(back[:, i, :], gated[:, i, :], identity[:])
             s = max(j for j, (a, b) in enumerate(SCATTERS) if a <= c * PIECE)
-            first = c * PIECE - SCATTERS[s][0]
+            start = c * PIECE - SCATTERS[s][0]
             nc.scalar.copy(
-                updates[s][:, first : first + PIECE], back[:].rearrange("p i n -> p (i n)")
+                updates[s][:, start : start + PIECE], back[:].rearrange("p i n -> p (i n)")
             )
 
         for (a, b), update in zip(SCATTERS, updates):

@@ -52,12 +52,16 @@ def tile_picked_modres_linrelu_l_kernel(
         halves = picked[:].bitcast(BF16).rearrange("p c u (n e) -> p c u n e", e=2)
 
         shared = pieces - 2
-        direct = keep.tile([P, PIECE * 4], BF16, name="grouped0", tag="grouped0", align_bytes=64)
-        low = keep.tile([P, PIECE], U32, name="low")
-        low_halves = low[:].bitcast(BF16).rearrange("p (n e) -> p n e", e=2)
-        quads = direct[:].rearrange("p (n j) -> p n j", j=4)
-        first = offsets[:, : PIECE // 16]
-        second = offsets[:, PIECE // 16 : 2 * PIECE // 16]
+        direct = [
+            keep.tile([P, PIECE * 4], BF16, name=f"grouped{c}", tag=f"grouped{c}", align_bytes=64)
+            for c in range(shared)
+        ]
+        early = [keep.tile([P, 2, PIECE], U32, name=f"early{c}") for c in range(shared)]
+        early_halves = [t[:].bitcast(BF16).rearrange("p u (n e) -> p u n e", e=2) for t in early]
+        for t in early:
+            nc.vector.memset(t[:, 1, :], 0)
+        own = [offsets[:, c * PIECE // 16 : (c + 1) * PIECE // 16] for c in range(shared)]
+
         lent = offsets[:, shared * PIECE // 16 :]
         for j in (0, 2, 1):
             plane = keep.tile([P, T], F32, name=f"plane{j}", align_bytes=256)
@@ -65,23 +69,28 @@ def tile_picked_modres_linrelu_l_kernel(
             if j == 0:
                 nc.sync.dma_start(offsets[:], offs)
             if j == 2:
-                nc.vector.tensor_copy(halves[:, 1, 1, :, 0], plane[:].indirect(second))
-                nc.vector.tensor_copy(quads[:, :, 2], plane[:].indirect(first))
+                for c in range(shared):
+                    nc.vector.tensor_copy(early_halves[c][:, 1, :, 0], plane[:].indirect(own[c]))
                 rounded = keep.tile([P, T], BF16, name="rounded2")
                 nc.scalar.copy(rounded[:], plane[:])
                 nc.scalar.activation(halves[:, shared:, 1, :, 0], rounded[:].indirect(lent), ACT.Copy)
             else:
-                nc.vector.tensor_copy(low_halves[:, :, j], plane[:].indirect(first))
-                nc.vector.tensor_copy(halves[:, 1:, 0, :, j], plane[:].indirect(offsets[:, PIECE // 16 :]))
-        nc.scalar.copy(direct[:].bitcast(U32).rearrange("p (n u) -> p n u", u=2)[:, :, 0], low[:])
+                for c in range(shared):
+                    nc.vector.tensor_copy(early_halves[c][:, 0, :, j], plane[:].indirect(own[c]))
+                nc.vector.tensor_copy(halves[:, shared:, 0, :, j], plane[:].indirect(lent))
+        for c in range(shared):
+            nc.gpsimd.tensor_copy(
+                direct[c][:].bitcast(U32).rearrange("p (n u) -> p n u", u=2), early[c][:].rearrange("p u n -> p n u")
+            )
 
-        late = keep.tile([P, T], F32, name="late", align_bytes=256)
+        late = keep.tile([P, T], F32, name="late", tag="late", align_bytes=256)
         rounded = keep.tile([P, T], BF16, name="rounded3")
         nc.sync.dma_start(late[:], rows[:, 3, :])
-        nc.scalar.copy(rounded[:, :576], late[:, :576])
-        nc.gpsimd.tensor_copy(rounded[:, 576:], late[:, 576:])
-        nc.vector.tensor_copy(halves[:, 1, 1, :, 1], late[:].indirect(second))
-        nc.vector.tensor_copy(quads[:, :, 3], late[:].indirect(first))
+        nc.scalar.copy(rounded[:, :1024], late[:, :1024])
+        nc.gpsimd.tensor_copy(rounded[:, 1024:], late[:, 1024:])
+        for c in range(shared):
+            quads = direct[c][:].rearrange("p (n j) -> p n j", j=4)
+            nc.vector.tensor_copy(quads[:, :, 3], late[:].indirect(own[c]))
 
         stream = keep.tile([P, T], F32, name="stream", align_bytes=256)
         nc.sync.dma_start(stream[:], res)
@@ -100,17 +109,12 @@ def tile_picked_modres_linrelu_l_kernel(
             nc.vector.quantize_mx(out=codes[:].bitcast(FP8X4), scales=scales[:], in_=grouped[:])
             return [(codes[:, a : a + PIECE], scales[:, a : a + PIECE]) for a in range(0, width, PIECE)]
 
-        grouped = keep.tile([P, PIECE * 4], BF16, name="grouped1", tag="grouped1", align_bytes=64)
-        nc.scalar.copy(
-            grouped[:].bitcast(U32).rearrange("p (n u) -> p n u", u=2),
-            picked[:, 1, :, :].rearrange("p u n -> p n u"),
-        )
-        quantised = quantise(0, direct, PIECE) + quantise(1, grouped, PIECE)
+        quantised = quantise(0, direct[0], PIECE) + quantise(1, direct[1], PIECE)
         for c in range(shared, pieces):
             entries = offsets[:, c * PIECE // 16 : (c + 1) * PIECE // 16]
             nc.scalar.activation(halves[:, c, 1, :, 1], rounded[:].indirect(entries), ACT.Copy)
-        old = picked[:, :2, :, :].rearrange("p c u n -> p (c u n)").bitcast(F32)
-        nc.vector.tensor_copy(old, stream[:].indirect(offsets[:]))
+        old = keep.tile([P, S], F32, name="old", tag="late", align_bytes=256)
+        nc.vector.tensor_copy(old[:], stream[:].indirect(offsets[:]))
         grouped = keep.tile([P, 2 * PIECE * 4], BF16, name="grouped2", tag="grouped1", align_bytes=64)
         for c in (2, 3):
             nc.gpsimd.tensor_copy(

@@ -32,7 +32,6 @@ def tile_picked_modres_linrelu_l_kernel(
         gate_rows = keep.tile([P, P], F32, name="gate_rows")
         nc.vector.memset(gate_rows[:], 0.0)
         w_scales = keep.tile([P, N], U8, name="w_scales", align_bytes=64)
-        nc.vector.memset(w_scales[:].bitcast(I32), 0)
         identity = keep.tile([P, P], F32, name="identity")
         make_identity(nc, identity[:])
 

@@ -139,18 +139,21 @@ def tile_picked_modres_linrelu_l_kernel(
             active = keep.tile([P, blocks, N], F32, name=f"active{c}")
             nc.scalar.activation(active[:], acc[:], ACT.Relu)
             gated = keep.tile([P, blocks, N], F32, name=f"gated{c}")
-            back = psum.tile([P, blocks, P], F32, name=f"back{c}", tag=f"bank{(2 * turn + 1 - turn // 2) % 4}")
-            for i in range(blocks):
-                b = c * blocks + i
-                nc.scalar.activation(
-                    gated[:, i, :], active[:, i, :], ACT.Copy, scale=gate_cols[:, b : b + 1]
-                )
-                nc.tensor.transpose(back[:, i, :], gated[:, i, :], identity[:])
             s = max(j for j, (a, b) in enumerate(SCATTERS) if a <= c * PIECE)
             start = c * PIECE - SCATTERS[s][0]
-            nc.scalar.copy(
-                updates[s][:, start : start + PIECE], back[:].rearrange("p i n -> p (i n)")
-            )
+            parts = [(0, 1), (1, 2)] if c % 2 else [(0, 2)]
+            for lo, hi in parts:
+                tag = f"bank{(2 * turn + 1 - turn // 2) % 4}" if hi == blocks else "bank4"
+                back = psum.tile([P, hi - lo, P], F32, name=f"back{c}_{lo}", tag=tag)
+                for i in range(lo, hi):
+                    b = c * blocks + i
+                    nc.scalar.activation(
+                        gated[:, i, :], active[:, i, :], ACT.Copy, scale=gate_cols[:, b : b + 1]
+                    )
+                    nc.tensor.transpose(back[:, i - lo, :], gated[:, i, :], identity[:])
+                nc.scalar.copy(
+                    updates[s][:, start + lo * P : start + hi * P], back[:].rearrange("p i n -> p (i n)")
+                )
 
         for (a, b), update in zip(SCATTERS, updates):
             nc.vector.tensor_tensor(

@@ -17,8 +17,7 @@ ALU = mybir.AluOpType
 ACT = mybir.ActivationFunctionType
 
 P = 128
-PIECE = 256
-SCATTERS = [(0, 512), (512, 1024)]
+PIECES = [(0, 256), (256, 640), (640, 1024)]
 
 
 def tile_picked_modres_linrelu_l_kernel(
@@ -27,136 +26,111 @@ def tile_picked_modres_linrelu_l_kernel(
     nc = tc.nc
     with ExitStack() as ctx:
         keep = ctx.enter_context(tc.tile_pool(name="keep", bufs=1))
+        swap = ctx.enter_context(tc.tile_pool(name="swap", bufs=1))
         psum = ctx.enter_context(tc.psum_pool(name="psum", bufs=1))
 
-        gate_rows = keep.tile([P, P], F32, name="gate_rows")
-        nc.vector.memset(gate_rows[:], 0.0)
-        w_scales = keep.tile([P, N], U8, name="w_scales", align_bytes=64)
         identity = keep.tile([P, P], F32, name="identity")
         make_identity(nc, identity[:])
-
+        w_scales = keep.tile([P, N], U8, name="w_scales", align_bytes=64)
         for q in range(4):
             nc.scalar.dma_start(
                 w_scales[32 * q : 32 * q + 4, :].bitcast(I32),
                 w1_scales[0, 4 * q : 4 * q + 4, :].bitcast(I32),
             )
-        nc.scalar.dma_start(gate_rows[: S // P, :], gate[0].rearrange("(b p) -> b p", p=P))
+        per = S // P
+        gate_cols = keep.tile([P, per], F32, name="gate_cols")
+        nc.scalar.dma_start(gate_cols[:], gate[0].rearrange("(p i) -> p i", i=per))
 
         offsets = keep.tile([P, S // 16], U16, name="offsets")
 
-        rows = xT.rearrange("(p j) t -> p j t", j=4)
-        pieces = S // PIECE
-        blocks = PIECE // P
-        picked = keep.tile([P, pieces, 2, PIECE], U32, name="picked", tag="picked")
-        halves = picked[:].bitcast(BF16).rearrange("p c u (n e) -> p c u n e", e=2)
+        def entries(a, b):
+            return offsets[:, a // 16 : b // 16]
 
-        shared = pieces - 2
-        direct = [
-            keep.tile([P, PIECE * 4], BF16, name=f"grouped{c}", tag=f"grouped{c}", align_bytes=64)
-            for c in range(shared)
-        ]
-        early = [keep.tile([P, 2, PIECE], U32, name=f"early{c}") for c in range(shared)]
+        rows = xT.rearrange("(p j) t -> p j t", j=4)
+        ahead = PIECES[:2]
+        quads = [keep.tile([P, (b - a) * 4], BF16, name=f"quads{a}", align_bytes=64) for a, b in ahead]
+        fourth = [t[:].rearrange("p (n j) -> p n j", j=4)[:, :, 3] for t in quads]
+        early = [keep.tile([P, 2, b - a], U32, name=f"early{a}") for a, b in ahead]
         early_halves = [t[:].bitcast(BF16).rearrange("p u (n e) -> p u n e", e=2) for t in early]
         for t in early:
             nc.vector.memset(t[:, 1, :], 0)
-        own = [offsets[:, c * PIECE // 16 : (c + 1) * PIECE // 16] for c in range(shared)]
+        a2, b2 = PIECES[2]
+        flat = keep.tile([P, 4, b2 - a2], BF16, name="flat")
 
-        lent = offsets[:, shared * PIECE // 16 :]
-        for j in (0, 2, 1):
+        w_codes = keep.tile([P, N], U32, name="w_codes", align_bytes=64)
+        for j in (0, 2, 1, 3):
             plane = keep.tile([P, T], F32, name=f"plane{j}", align_bytes=256)
             nc.sync.dma_start(plane[:], rows[:, j, :])
             if j == 0:
                 nc.sync.dma_start(offsets[:], offs)
-            if j == 2:
-                for c in range(shared):
-                    nc.vector.tensor_copy(early_halves[c][:, 1, :, 0], plane[:].indirect(own[c]))
-                rounded = keep.tile([P, T], BF16, name="rounded2")
-                nc.scalar.copy(rounded[:], plane[:])
-                nc.scalar.activation(halves[:, shared:, 1, :, 0], rounded[:].indirect(lent), ACT.Copy)
+            if j == 3:
+                for c in range(2):
+                    nc.gpsimd.tensor_copy(
+                        quads[c][:].bitcast(U32).rearrange("p (n u) -> p n u", u=2),
+                        early[c][:].rearrange("p u n -> p n u"),
+                    )
+                nc.vector.tensor_copy(fourth[0], plane[:].indirect(entries(*PIECES[0])))
+                lent = keep.tile([P, PIECES[1][1] - PIECES[1][0]], BF16, name="lent")
+                nc.scalar.activation(lent[:], plane[:].indirect(entries(*PIECES[1])), ACT.Copy)
+                nc.vector.tensor_copy(fourth[1], lent[:])
             else:
-                for c in range(shared):
-                    nc.vector.tensor_copy(early_halves[c][:, 0, :, j], plane[:].indirect(own[c]))
-                nc.vector.tensor_copy(halves[:, shared:, 0, :, j], plane[:].indirect(lent))
-        for c in range(shared):
-            nc.gpsimd.tensor_copy(
-                direct[c][:].bitcast(U32).rearrange("p (n u) -> p n u", u=2), early[c][:].rearrange("p u n -> p n u")
-            )
-
-        late = keep.tile([P, T], F32, name="late", tag="late", align_bytes=256)
-        rounded = keep.tile([P, T], BF16, name="rounded3")
-        nc.sync.dma_start(late[:], rows[:, 3, :])
-        nc.scalar.copy(rounded[:, :1024], late[:, :1024])
-        nc.gpsimd.tensor_copy(rounded[:, 1024:], late[:, 1024:])
-        for c in range(shared):
-            quads = direct[c][:].rearrange("p (n j) -> p n j", j=4)
-            nc.vector.tensor_copy(quads[:, :, 3], late[:].indirect(own[c]))
-
-        stream = keep.tile([P, T], F32, name="stream", align_bytes=256)
-        nc.sync.dma_start(stream[:], res)
-        gate_turned = psum.tile([P, P], F32, name="gate_turned")
-        nc.tensor.transpose(gate_turned[:], gate_rows[:], identity[:])
-        gate_cols = keep.tile([P, S // P], F32, name="gate_cols")
-        nc.scalar.copy(gate_cols[:], gate_turned[:, : S // P])
-        w_codes = keep.tile([P, N], U32, name="w_codes", align_bytes=64)
+                for c, (a, b) in enumerate(ahead):
+                    nc.vector.tensor_copy(early_halves[c][:, j // 2, :, j % 2], plane[:].indirect(entries(a, b)))
+            nc.scalar.activation(flat[:, j, :], plane[:].indirect(entries(a2, b2)), ACT.Copy)
+            if j == 0:
+                gate_all = keep.tile([P, P, per], F32, name="gate_all")
+                for h in range(2):
+                    spread = psum.tile([P, 4, P], F32, name=f"spread{h}")
+                    for i in range(4):
+                        col = gate_cols[:, 4 * h + i : 4 * h + i + 1]
+                        nc.tensor.transpose(spread[:, i, :], col.to_broadcast([P, P]), identity[:])
+                    nc.scalar.copy(gate_all[:, :, 4 * h : 4 * h + 4], spread[:].rearrange("p i n -> p n i"))
         nc.sync.dma_start(
             w_codes[:].bitcast(I32), w1_words[0].rearrange("p n t -> p (n t)").bitcast(I32)
         )
+        stream = keep.tile([P, T], F32, name="stream", align_bytes=256)
+        nc.sync.dma_start(stream[:], res)
+        gates = gate_all[:].rearrange("p n i -> p (n i)")
 
-        def quantise(name, grouped, width):
-            codes = keep.tile([P, width], U32, name=f"codes{name}", align_bytes=64)
-            scales = keep.tile([P, width], U8, name=f"scales{name}", align_bytes=64)
-            nc.vector.quantize_mx(out=codes[:].bitcast(FP8X4), scales=scales[:], in_=grouped[:])
-            return [(codes[:, a : a + PIECE], scales[:, a : a + PIECE]) for a in range(0, width, PIECE)]
+        cut = 384
+        old = keep.tile([P, S], F32, name="old")
+        nc.scalar.activation(old[:, cut:], stream[:].indirect(entries(cut, S)), ACT.Copy)
+        update_at = [2560, 3072, 4608]
 
-        quantised = quantise(0, direct[0], PIECE) + quantise(1, direct[1], PIECE)
-        for c in range(shared, pieces):
-            entries = offsets[:, c * PIECE // 16 : (c + 1) * PIECE // 16]
-            nc.scalar.activation(halves[:, c, 1, :, 1], rounded[:].indirect(entries), ACT.Copy)
-        old = keep.tile([P, S], F32, name="old", tag="late", align_bytes=256)
-        nc.vector.tensor_copy(old[:], stream[:].indirect(offsets[:]))
-        grouped = keep.tile([P, 2 * PIECE * 4], BF16, name="grouped2", tag="grouped1", align_bytes=64)
-        for c in (2, 3):
-            nc.gpsimd.tensor_copy(
-                grouped[:, (c - 2) * PIECE * 4 : (c - 1) * PIECE * 4].bitcast(U32).rearrange("p (n u) -> p n u", u=2),
-                picked[:, c, :, :].rearrange("p u n -> p n u"),
-            )
-        quantised.extend(quantise(2, grouped, 2 * PIECE))
-
-        updates = [keep.tile([P, b - a], F32, name=f"update{a}") for a, b in SCATTERS]
-        for turn, (c, (codes, scales)) in enumerate(zip((0, 1, 2, 3), quantised)):
-            acc = psum.tile([P, blocks, N], F32, name=f"acc{c}", tag=f"bank{(2 * turn + turn // 2) % 4}")
-            for i in range(blocks):
-                cols = slice(i * P, (i + 1) * P)
+        news = []
+        for c, (a, b) in enumerate(PIECES):
+            n = b - a
+            if c == 2:
+                woven = swap.tile([P, n * 4], BF16, name="quads2", offset=0, align_bytes=64)
+                nc.vector.tensor_copy(
+                    woven[:].rearrange("p (c i t) -> p c t i", i=4, t=4),
+                    flat[:].rearrange("p t (c i) -> p c t i", i=4),
+                )
+            else:
+                woven = quads[c]
+            codes = keep.tile([P, n], U32, name=f"codes{c}", align_bytes=64)
+            scales = keep.tile([P, n], U8, name=f"scales{c}", align_bytes=64)
+            nc.vector.quantize_mx(out=codes[:].bitcast(FP8X4), scales=scales[:], in_=woven[:])
+            acc = psum.tile([P, n], F32, name=f"acc{c}")
+            for lo in range(0, n, 256):
+                cols = slice(lo, min(lo + 256, n))
                 nc.tensor.matmul_mx(
-                    out=acc[:, i, :],
-                    lhsT=codes[:, cols].bitcast(FP8X4),
-                    lhsT_scale=scales[:, cols],
-                    rhs=w_codes[:].bitcast(FP8X4),
-                    rhs_scale=w_scales[:],
+                    out=acc[:, cols],
+                    lhsT=w_codes[:].bitcast(FP8X4),
+                    lhsT_scale=w_scales[:],
+                    rhs=codes[:, cols].bitcast(FP8X4),
+                    rhs_scale=scales[:, cols],
                     start=True,
                     stop=True,
                 )
-            active = keep.tile([P, blocks, N], F32, name=f"active{c}")
-            nc.scalar.activation(active[:], acc[:], ACT.Relu)
-            gated = keep.tile([P, blocks, N], F32, name=f"gated{c}")
-            s = max(j for j, (a, b) in enumerate(SCATTERS) if a <= c * PIECE)
-            start = c * PIECE - SCATTERS[s][0]
-            parts = [(0, 1), (1, 2)] if c % 2 else [(0, 2)]
-            for lo, hi in parts:
-                tag = f"bank{(2 * turn + 1 - turn // 2) % 4}" if hi == blocks else "bank4"
-                back = psum.tile([P, hi - lo, P], F32, name=f"back{c}_{lo}", tag=tag)
-                for i in range(lo, hi):
-                    b = c * blocks + i
-                    nc.scalar.activation(
-                        gated[:, i, :], active[:, i, :], ACT.Copy, scale=gate_cols[:, b : b + 1]
-                    )
-                    nc.tensor.transpose(back[:, i - lo, :], gated[:, i, :], identity[:])
-                nc.scalar.copy(
-                    updates[s][:, start + lo * P : start + hi * P], back[:].rearrange("p i n -> p (i n)")
-                )
-
-        for (a, b), update in zip(SCATTERS, updates):
-            nc.vector.tensor_tensor(
-                stream[:].indirect(offsets[:, a // 16 : b // 16]), old[:, a:b], update[:], ALU.add
-            )
+            update = swap.tile([P, n], F32, name=f"update{c}", offset=update_at[c], align_bytes=64)
+            nc.vector.scalar_tensor_tensor(update[:], acc[:], 0.0, gates[:, a:b], ALU.max, ALU.mult)
+            if c == 0:
+                nc.vector.tensor_copy(old[:, :b], stream[:].indirect(entries(0, b)))
+                nc.vector.tensor_copy(old[:, b:cut], stream[:].indirect(entries(b, cut)))
+            new = keep.tile([P, n], F32, name=f"new{c}")
+            nc.vector.tensor_tensor(new[:], old[:, a:b], update[:], ALU.add)
+            news.append(new)
+        for (a, b), new in zip(PIECES, news):
+            nc.scalar.activation(stream[:].indirect(entries(a, b)), new[:], ACT.Copy)
         nc.sync.dma_start(out, stream[:])

@@ -108,7 +108,7 @@ def tile_picked_modres_linrelu_l_kernel(
                 )
             else:
                 woven = quads[c]
-            codes = keep.tile([P, n], U32, name=f"codes{c}", align_bytes=64)
+            codes = keep.tile([P, n], U32, name=f"codes{c}", tag=f"codes{c // 2}", align_bytes=64)
             scales = keep.tile([P, n], U8, name=f"scales{c}", align_bytes=64)
             nc.vector.quantize_mx(out=codes[:].bitcast(FP8X4), scales=scales[:], in_=woven[:])
             acc = psum.tile([P, n], F32, name=f"acc{c}")
@@ -125,12 +125,16 @@ def tile_picked_modres_linrelu_l_kernel(
                 )
             update = swap.tile([P, n], F32, name=f"update{c}", offset=update_at[c], align_bytes=64)
             nc.vector.scalar_tensor_tensor(update[:], acc[:], 0.0, gates[:, a:b], ALU.max, ALU.mult)
-            if c == 0:
-                nc.vector.tensor_copy(old[:, :b], stream[:].indirect(entries(0, b)))
-                nc.vector.tensor_copy(old[:, b:cut], stream[:].indirect(entries(b, cut)))
+            if c == 2:
+                break
             new = keep.tile([P, n], F32, name=f"new{c}")
-            nc.vector.tensor_tensor(new[:], old[:, a:b], update[:], ALU.add)
+            if c == 0:
+                nc.vector.tensor_tensor(new[:], stream[:].indirect(entries(a, b)), update[:], ALU.add)
+                nc.vector.tensor_copy(old[:, b:cut], stream[:].indirect(entries(b, cut)))
+            else:
+                nc.vector.tensor_tensor(new[:], old[:, a:b], update[:], ALU.add)
             news.append(new)
-        for (a, b), new in zip(PIECES, news):
+        for (a, b), new in zip(PIECES[:2], news):
             nc.scalar.activation(stream[:].indirect(entries(a, b)), new[:], ACT.Copy)
+        nc.vector.tensor_tensor(stream[:].indirect(entries(a2, b2)), old[:, a2:b2], update[:], ALU.add)
         nc.sync.dma_start(out, stream[:])

@@ -49,11 +49,12 @@ def tile_picked_modres_linrelu_l_kernel(
         rows = xT.rearrange("(p j) t -> p j t", j=4)
         ahead = PIECES[:2]
         quads = [keep.tile([P, (b - a) * 4], BF16, name=f"quads{a}", align_bytes=64) for a, b in ahead]
-        fourth = [t[:].rearrange("p (n j) -> p n j", j=4)[:, :, 3] for t in quads]
+        slots = [t[:].rearrange("p (n j) -> p n j", j=4) for t in quads]
+        fourth = [t[:, :, 3] for t in slots]
         early = [keep.tile([P, 2, b - a], U32, name=f"early{a}") for a, b in ahead]
         early_halves = [t[:].bitcast(BF16).rearrange("p u (n e) -> p u n e", e=2) for t in early]
         for t in early:
-            nc.vector.memset(t[:, 1, :], 0)
+            nc.vector.memset(t[:], 0)
         a2, b2 = PIECES[2]
         flat = keep.tile([P, 4, b2 - a2], BF16, name="flat")
 
@@ -64,15 +65,18 @@ def tile_picked_modres_linrelu_l_kernel(
             if j == 0:
                 nc.sync.dma_start(offsets[:], offs)
             if j == 3:
+                nc.vector.tensor_copy(fourth[0], plane[:].indirect(entries(*PIECES[0])))
+                lent = keep.tile([P, PIECES[1][1] - PIECES[1][0]], BF16, name="lent")
+                nc.scalar.activation(lent[:], plane[:].indirect(entries(*PIECES[1])), ACT.Copy)
+                nc.vector.tensor_copy(fourth[1], lent[:])
+            elif j == 1:
                 for c in range(2):
                     nc.gpsimd.tensor_copy(
                         quads[c][:].bitcast(U32).rearrange("p (n u) -> p n u", u=2),
                         early[c][:].rearrange("p u n -> p n u"),
                     )
-                nc.vector.tensor_copy(fourth[0], plane[:].indirect(entries(*PIECES[0])))
-                lent = keep.tile([P, PIECES[1][1] - PIECES[1][0]], BF16, name="lent")
-                nc.scalar.activation(lent[:], plane[:].indirect(entries(*PIECES[1])), ACT.Copy)
-                nc.vector.tensor_copy(fourth[1], lent[:])
+                for c, (a, b) in enumerate(ahead):
+                    nc.vector.tensor_copy(slots[c][:, :, 1], plane[:].indirect(entries(a, b)))
             else:
                 for c, (a, b) in enumerate(ahead):
                     nc.vector.tensor_copy(early_halves[c][:, j // 2, :, j % 2], plane[:].indirect(entries(a, b)))
@@ -92,26 +96,17 @@ def tile_picked_modres_linrelu_l_kernel(
         nc.sync.dma_start(stream[:], res)
         gates = gate_all[:].rearrange("p n i -> p (n i)")
 
-        cut = 384
-        old = keep.tile([P, S], F32, name="old")
-        nc.scalar.activation(old[:, cut:], stream[:].indirect(entries(cut, S)), ACT.Copy)
-        update_at = [2560, 3072, 4608]
+        cut = 256
 
-        news = []
-        for c, (a, b) in enumerate(PIECES):
+        old = keep.tile([P, S], F32, name="old")
+        nc.scalar.activation(old[:, cut:S], stream[:].indirect(entries(cut, S)), ACT.Copy)
+
+        def product(name, source, a, b, update, tag):
             n = b - a
-            if c == 2:
-                woven = swap.tile([P, n * 4], BF16, name="quads2", offset=0, align_bytes=64)
-                nc.vector.tensor_copy(
-                    woven[:].rearrange("p (c i t) -> p c t i", i=4, t=4),
-                    flat[:].rearrange("p t (c i) -> p c t i", i=4),
-                )
-            else:
-                woven = quads[c]
-            codes = keep.tile([P, n], U32, name=f"codes{c}", tag=f"codes{c // 2}", align_bytes=64)
-            scales = keep.tile([P, n], U8, name=f"scales{c}", align_bytes=64)
-            nc.vector.quantize_mx(out=codes[:].bitcast(FP8X4), scales=scales[:], in_=woven[:])
-            acc = psum.tile([P, n], F32, name=f"acc{c}")
+            codes = keep.tile([P, n], U32, name=f"codes{name}", tag=tag, align_bytes=64)
+            scales = keep.tile([P, n], U8, name=f"scales{name}", align_bytes=64)
+            nc.vector.quantize_mx(out=codes[:].bitcast(FP8X4), scales=scales[:], in_=source)
+            acc = psum.tile([P, n], F32, name=f"acc{name}")
             for lo in range(0, n, 256):
                 cols = slice(lo, min(lo + 256, n))
                 nc.tensor.matmul_mx(
@@ -123,18 +118,32 @@ def tile_picked_modres_linrelu_l_kernel(
                     start=True,
                     stop=True,
                 )
-            update = swap.tile([P, n], F32, name=f"update{c}", offset=update_at[c], align_bytes=64)
-            nc.vector.scalar_tensor_tensor(update[:], acc[:], 0.0, gates[:, a:b], ALU.max, ALU.mult)
-            if c == 2:
-                break
-            new = keep.tile([P, n], F32, name=f"new{c}")
+            nc.vector.scalar_tensor_tensor(update, acc[:], 0.0, gates[:, a:b], ALU.max, ALU.mult)
+
+        news = []
+        for c, (a, b) in enumerate(ahead):
+            update = swap.tile([P, b - a], F32, name=f"update{c}", offset=(2560, 3072)[c], align_bytes=64)
+            product(c, quads[c][:], a, b, update[:], "codes_ahead")
+            new = keep.tile([P, b - a], F32, name=f"new{c}")
             if c == 0:
                 nc.vector.tensor_tensor(new[:], stream[:].indirect(entries(a, b)), update[:], ALU.add)
-                nc.vector.tensor_copy(old[:, b:cut], stream[:].indirect(entries(b, cut)))
+
             else:
                 nc.vector.tensor_tensor(new[:], old[:, a:b], update[:], ALU.add)
             news.append(new)
-        for (a, b), new in zip(PIECES[:2], news):
+
+        woven = swap.tile([P, (b2 - a2) * 4], BF16, name="quads2", offset=0, align_bytes=64)
+        late = keep.tile([P, b2 - a2], F32, name="late")
+
+        for a, b in ((640,768,),(768,1024,),):
+            source = woven[:, (a - a2) * 4 : (b - a2) * 4]
+            nc.vector.tensor_copy(
+                source.rearrange("p (c i t) -> p c t i", i=4, t=4),
+                flat[:, :, a - a2 : b - a2].rearrange("p t (c i) -> p c t i", i=4),
+            )
+            product(a, source, a, b, late[:, a - a2 : b - a2], f"codes{a}")
+
+        for (a, b), new in zip(ahead, news):
             nc.scalar.activation(stream[:].indirect(entries(a, b)), new[:], ACT.Copy)
-        nc.vector.tensor_tensor(stream[:].indirect(entries(a2, b2)), old[:, a2:b2], update[:], ALU.add)
+        nc.vector.tensor_tensor(stream[:].indirect(entries(a2, b2)), old[:, a2:b2], late[:], ALU.add)
         nc.sync.dma_start(out, stream[:])

@@ -97,9 +97,10 @@ def tile_picked_modres_linrelu_l_kernel(
         gates = gate_all[:].rearrange("p n i -> p (n i)")
 
         cut = 256
-
+        again = keep.tile([P, T], F32, name="again", align_bytes=256)
+        nc.sync.dma_start(again[:], res)
         old = keep.tile([P, S], F32, name="old")
-        nc.scalar.activation(old[:, cut:S], stream[:].indirect(entries(cut, S)), ACT.Copy)
+        nc.scalar.activation(old[:, cut:832], stream[:].indirect(entries(cut, 832)), ACT.Copy)
 
         def product(name, source, a, b, update, tag):
             n = b - a
@@ -134,7 +135,7 @@ def tile_picked_modres_linrelu_l_kernel(
 
         woven = swap.tile([P, (b2 - a2) * 4], BF16, name="quads2", offset=0, align_bytes=64)
         late = keep.tile([P, b2 - a2], F32, name="late")
-
+        nc.vector.tensor_copy(old[:, 832:], again[:].indirect(entries(832, b2)))
         for a, b in ((640,768,),(768,1024,),):
             source = woven[:, (a - a2) * 4 : (b - a2) * 4]
             nc.vector.tensor_copy(

@@ -38,8 +38,9 @@ def tile_picked_modres_linrelu_l_kernel(
                 w1_scales[0, 4 * q : 4 * q + 4, :].bitcast(I32),
             )
         per = S // P
-        gate_cols = keep.tile([P, per], F32, name="gate_cols")
-        nc.scalar.dma_start(gate_cols[:], gate[0].rearrange("(p i) -> p i", i=per))
+        gate_rows = keep.tile([P, P], F32, name="gate_rows")
+        nc.vector.memset(gate_rows[:], 0.0)
+        nc.scalar.dma_start(gate_rows[:per, :], gate[0].rearrange("(b p) -> b p", p=P))
 
         offsets = keep.tile([P, S // 16], U16, name="offsets")
 
@@ -53,8 +54,8 @@ def tile_picked_modres_linrelu_l_kernel(
         fourth = [t[:, :, 3] for t in slots]
         early = [keep.tile([P, 2, b - a], U32, name=f"early{a}") for a, b in ahead]
         early_halves = [t[:].bitcast(BF16).rearrange("p u (n e) -> p u n e", e=2) for t in early]
-        for t in early:
-            nc.vector.memset(t[:], 0)
+        nc.vector.memset(early[1][:], 0)
+        nc.scalar.copy(early[0][:], early[1][:, :, : PIECES[0][1]])
         a2, b2 = PIECES[2]
         flat = keep.tile([P, 4, b2 - a2], BF16, name="flat")
 
@@ -68,7 +69,7 @@ def tile_picked_modres_linrelu_l_kernel(
                 nc.vector.tensor_copy(fourth[0], plane[:].indirect(entries(*PIECES[0])))
                 lent = keep.tile([P, PIECES[1][1] - PIECES[1][0]], BF16, name="lent")
                 nc.scalar.activation(lent[:], plane[:].indirect(entries(*PIECES[1])), ACT.Copy)
-                nc.vector.tensor_copy(fourth[1], lent[:])
+                nc.vector.tensor_copy(fourth[1][:, :256], lent[:, :256])
             elif j == 1:
                 for c in range(2):
                     nc.gpsimd.tensor_copy(
@@ -81,14 +82,20 @@ def tile_picked_modres_linrelu_l_kernel(
                 for c, (a, b) in enumerate(ahead):
                     nc.vector.tensor_copy(early_halves[c][:, j // 2, :, j % 2], plane[:].indirect(entries(a, b)))
             nc.scalar.activation(flat[:, j, :], plane[:].indirect(entries(a2, b2)), ACT.Copy)
+            if j == 3:
+                nc.scalar.copy(fourth[1][:, 256:], lent[:, 256:])
             if j == 0:
-                gate_all = keep.tile([P, P, per], F32, name="gate_all")
+                gate_all = keep.tile([P, per, P], F32, name="gate_all")
+                turned = psum.tile([P, P], F32, name="turned")
+                nc.tensor.transpose(turned[:], gate_rows[:], identity[:])
+                gate_cols = keep.tile([P, per], F32, name="gate_cols")
+                nc.scalar.copy(gate_cols[:], turned[:, :per])
                 for h in range(2):
                     spread = psum.tile([P, 4, P], F32, name=f"spread{h}")
                     for i in range(4):
                         col = gate_cols[:, 4 * h + i : 4 * h + i + 1]
                         nc.tensor.transpose(spread[:, i, :], col.to_broadcast([P, P]), identity[:])
-                    nc.scalar.copy(gate_all[:, :, 4 * h : 4 * h + 4], spread[:].rearrange("p i n -> p n i"))
+                    nc.scalar.copy(gate_all[:, 4 * h : 4 * h + 4, :], spread[:])
         nc.sync.dma_start(
             w_codes[:].bitcast(I32), w1_words[0].rearrange("p n t -> p (n t)").bitcast(I32)
         )
@@ -102,12 +109,15 @@ def tile_picked_modres_linrelu_l_kernel(
         old = keep.tile([P, S], F32, name="old")
         nc.scalar.activation(old[:, cut:832], stream[:].indirect(entries(cut, 832)), ACT.Copy)
 
-        def product(name, source, a, b, update, tag):
+        def multiply(name, source, a, b, tag, held=False):
             n = b - a
             codes = keep.tile([P, n], U32, name=f"codes{name}", tag=tag, align_bytes=64)
-            scales = keep.tile([P, n], U8, name=f"scales{name}", align_bytes=64)
+            if held:
+                scales = swap.tile([P, n], U8, name=f"scales{name}", offset=3200, align_bytes=64)
+            else:
+                scales = keep.tile([P, n], U8, name=f"scales{name}", align_bytes=64)
             nc.vector.quantize_mx(out=codes[:].bitcast(FP8X4), scales=scales[:], in_=source)
-            acc = psum.tile([P, n], F32, name=f"acc{name}")
+            acc = psum.tile([P, n], F32, name=f"acc{name}", tag="turned" if a == 0 else f"acc{name}")
             for lo in range(0, n, 256):
                 cols = slice(lo, min(lo + 256, n))
                 nc.tensor.matmul_mx(
@@ -119,25 +129,40 @@ def tile_picked_modres_linrelu_l_kernel(
                     start=True,
                     stop=True,
                 )
+            return acc
+
+        def gated(update, acc, a, b):
             nc.vector.scalar_tensor_tensor(update, acc[:], 0.0, gates[:, a:b], ALU.max, ALU.mult)
 
-        news = []
-        for c, (a, b) in enumerate(ahead):
-            update = swap.tile([P, b - a], F32, name=f"update{c}", offset=(2560, 3072)[c], align_bytes=64)
-            product(c, quads[c][:], a, b, update[:], "codes_ahead")
-            new = keep.tile([P, b - a], F32, name=f"new{c}")
-            if c == 0:
-                nc.vector.tensor_tensor(new[:], stream[:].indirect(entries(a, b)), update[:], ALU.add)
+        def product(name, source, a, b, update, tag):
+            gated(update, multiply(name, source, a, b, tag), a, b)
 
-            else:
-                nc.vector.tensor_tensor(new[:], old[:, a:b], update[:], ALU.add)
-            news.append(new)
+        a0, b0 = PIECES[0]
+        a1, b1 = PIECES[1]
+        mid = (a0 + b0) // 2
+        news = [keep.tile([P, b - a], F32, name=f"new{a}") for a, b in ahead]
+        updates = [
+            swap.tile([P, mid - a0], F32, name="update0", offset=3072, align_bytes=64),
+            keep.tile([P, b0 - mid], F32, name="update0b"),
+        ]
+        product(0, quads[0][:, : 4 * mid], a0, mid, updates[0][:], "codes0")
+        product(mid, quads[0][:, 4 * mid :], mid, b0, updates[1][:], "codes_ahead")
+        update = swap.tile([P, b1 - a1], F32, name="update1", offset=3520, align_bytes=64)
+        for (a, b), part in zip(((a0, mid), (mid, b0)), updates):
+            nc.vector.tensor_tensor(news[0][:, a:b], stream[:].indirect(entries(a, b)), part[:], ALU.add)
+        sums = [
+            multiply(a1, quads[1][:, :1024], a1, 512, "codes_ahead"),
+            multiply(512, quads[1][:, 1024:], 512, b1, "codes512", held=True),
+        ]
+        gated(update[:, :256], sums[0], a1, 512)
+        gated(update[:, 256:], sums[1], 512, b1)
+        nc.vector.tensor_tensor(news[1][:], old[:, a1:b1], update[:], ALU.add)
 
-        woven = swap.tile([P, (b2 - a2) * 4], BF16, name="quads2", offset=0, align_bytes=64)
         late = keep.tile([P, b2 - a2], F32, name="late")
         nc.vector.tensor_copy(old[:, 832:], again[:].indirect(entries(832, b2)))
-        for a, b in ((640,768,),(768,1024,),):
-            source = woven[:, (a - a2) * 4 : (b - a2) * 4]
+        for a, b in ((640,896,),(896,1024,),):
+            woven = swap.tile([P, (b - a) * 4], BF16, name=f"quads{a}", offset=1088 if a == a2 else 4992, align_bytes=64)
+            source = woven[:]
             nc.vector.tensor_copy(
                 source.rearrange("p (c i t) -> p c t i", i=4, t=4),
                 flat[:, :, a - a2 : b - a2].rearrange("p t (c i) -> p c t i", i=4),

@@ -103,11 +103,9 @@ def tile_picked_modres_linrelu_l_kernel(
         nc.sync.dma_start(stream[:], res)
         gates = gate_all[:].rearrange("p n i -> p (n i)")
 
-        cut = 256
-        again = keep.tile([P, T], F32, name="again", align_bytes=256)
-        nc.sync.dma_start(again[:], res)
+        cut = 384
         old = keep.tile([P, S], F32, name="old")
-        nc.scalar.activation(old[:, cut:832], stream[:].indirect(entries(cut, 832)), ACT.Copy)
+        nc.scalar.activation(old[:, cut:], stream[:].indirect(entries(cut, S)), ACT.Copy)
 
         def multiply(name, source, a, b, tag, held=False):
             n = b - a
@@ -150,6 +148,7 @@ def tile_picked_modres_linrelu_l_kernel(
         update = swap.tile([P, b1 - a1], F32, name="update1", offset=3520, align_bytes=64)
         for (a, b), part in zip(((a0, mid), (mid, b0)), updates):
             nc.vector.tensor_tensor(news[0][:, a:b], stream[:].indirect(entries(a, b)), part[:], ALU.add)
+        nc.vector.tensor_copy(old[:, a1:cut], stream[:].indirect(entries(a1, cut)))
         sums = [
             multiply(a1, quads[1][:, :1024], a1, 512, "codes_ahead"),
             multiply(512, quads[1][:, 1024:], 512, b1, "codes512", held=True),
@@ -159,7 +158,6 @@ def tile_picked_modres_linrelu_l_kernel(
         nc.vector.tensor_tensor(news[1][:], old[:, a1:b1], update[:], ALU.add)
 
         late = keep.tile([P, b2 - a2], F32, name="late")
-        nc.vector.tensor_copy(old[:, 832:], again[:].indirect(entries(832, b2)))
         for a, b in ((640,896,),(896,1024,),):
             woven = swap.tile([P, (b - a) * 4], BF16, name=f"quads{a}", offset=1088 if a == a2 else 4992, align_bytes=64)
             source = woven[:]

@@ -103,9 +103,11 @@ def tile_picked_modres_linrelu_l_kernel(
         nc.sync.dma_start(stream[:], res)
         gates = gate_all[:].rearrange("p n i -> p (n i)")
 
-        cut = 384
+        cut = 256
+        again = keep.tile([P, T], F32, name="again", tag="plane3", align_bytes=256)
+        nc.sync.dma_start(again[:], res)
         old = keep.tile([P, S], F32, name="old")
-        nc.scalar.activation(old[:, cut:], stream[:].indirect(entries(cut, S)), ACT.Copy)
+        nc.scalar.activation(old[:, cut:768], stream[:].indirect(entries(cut, 768)), ACT.Copy)
 
         def multiply(name, source, a, b, tag, held=False):
             n = b - a
@@ -115,7 +117,7 @@ def tile_picked_modres_linrelu_l_kernel(
             else:
                 scales = keep.tile([P, n], U8, name=f"scales{name}", align_bytes=64)
             nc.vector.quantize_mx(out=codes[:].bitcast(FP8X4), scales=scales[:], in_=source)
-            acc = psum.tile([P, n], F32, name=f"acc{name}", tag="turned" if a == 0 else f"acc{name}")
+            acc = psum.tile([P, n], F32, name=f"acc{name}", tag={0: "turned", 896: "spread0"}.get(a, f"acc{name}"))
             for lo in range(0, n, 256):
                 cols = slice(lo, min(lo + 256, n))
                 nc.tensor.matmul_mx(
@@ -148,7 +150,6 @@ def tile_picked_modres_linrelu_l_kernel(
         update = swap.tile([P, b1 - a1], F32, name="update1", offset=3520, align_bytes=64)
         for (a, b), part in zip(((a0, mid), (mid, b0)), updates):
             nc.vector.tensor_tensor(news[0][:, a:b], stream[:].indirect(entries(a, b)), part[:], ALU.add)
-        nc.vector.tensor_copy(old[:, a1:cut], stream[:].indirect(entries(a1, cut)))
         sums = [
             multiply(a1, quads[1][:, :1024], a1, 512, "codes_ahead"),
             multiply(512, quads[1][:, 1024:], 512, b1, "codes512", held=True),
@@ -158,8 +159,9 @@ def tile_picked_modres_linrelu_l_kernel(
         nc.vector.tensor_tensor(news[1][:], old[:, a1:b1], update[:], ALU.add)
 
         late = keep.tile([P, b2 - a2], F32, name="late")
-        for a, b in ((640,896,),(896,1024,),):
-            woven = swap.tile([P, (b - a) * 4], BF16, name=f"quads{a}", offset=1088 if a == a2 else 4992, align_bytes=64)
+        nc.vector.tensor_copy(old[:, 768:], again[:].indirect(entries(768, b2)))
+        for a, b in ((640, 768), (768, 896), (896, 1024)):
+            woven = swap.tile([P, (b - a) * 4], BF16, name=f"quads{a}", offset={640: 2112, 768: 4992, 896: 3584}[a], align_bytes=64)
             source = woven[:]
             nc.vector.tensor_copy(
                 source.rearrange("p (c i t) -> p c t i", i=4, t=4),

@@ -31,16 +31,15 @@ def tile_picked_modres_linrelu_l_kernel(
 
         identity = keep.tile([P, P], F32, name="identity")
         make_identity(nc, identity[:])
+        per = S // P
+        gate_cols = keep.tile([P, per], F32, name="gate_cols")
+        nc.scalar.dma_start(gate_cols[:], gate[0].rearrange("(p b) -> p b", b=per))
         w_scales = keep.tile([P, N], U8, name="w_scales", align_bytes=64)
         for q in range(4):
             nc.scalar.dma_start(
                 w_scales[32 * q : 32 * q + 4, :].bitcast(I32),
                 w1_scales[0, 4 * q : 4 * q + 4, :].bitcast(I32),
             )
-        per = S // P
-        gate_rows = keep.tile([P, P], F32, name="gate_rows")
-        nc.vector.memset(gate_rows[:], 0.0)
-        nc.scalar.dma_start(gate_rows[:per, :], gate[0].rearrange("(b p) -> b p", p=P))
 
         offsets = keep.tile([P, S // 16], U16, name="offsets")
 
@@ -76,8 +75,10 @@ def tile_picked_modres_linrelu_l_kernel(
                         quads[c][:].bitcast(U32).rearrange("p (n u) -> p n u", u=2),
                         early[c][:].rearrange("p u n -> p n u"),
                     )
-                for c, (a, b) in enumerate(ahead):
-                    nc.vector.tensor_copy(slots[c][:, :, 1], plane[:].indirect(entries(a, b)))
+                nc.vector.tensor_copy(slots[0][:, :, 1], plane[:].indirect(entries(*PIECES[0])))
+                lent_early = keep.tile([P, PIECES[1][1] - PIECES[1][0]], BF16, name="lent_early")
+                nc.scalar.activation(lent_early[:], plane[:].indirect(entries(*PIECES[1])), ACT.Copy)
+                nc.vector.tensor_copy(slots[1][:, :, 1], lent_early[:])
             else:
                 for c, (a, b) in enumerate(ahead):
                     nc.vector.tensor_copy(early_halves[c][:, j // 2, :, j % 2], plane[:].indirect(entries(a, b)))
@@ -85,17 +86,13 @@ def tile_picked_modres_linrelu_l_kernel(
             if j == 3:
                 nc.scalar.copy(fourth[1][:, 256:], lent[:, 256:])
             if j == 0:
-                gate_all = keep.tile([P, per, P], F32, name="gate_all")
-                turned = psum.tile([P, P], F32, name="turned")
-                nc.tensor.transpose(turned[:], gate_rows[:], identity[:])
-                gate_cols = keep.tile([P, per], F32, name="gate_cols")
-                nc.scalar.copy(gate_cols[:], turned[:, :per])
+                gate_all = keep.tile([P, P, per], F32, name="gate_all")
                 for h in range(2):
                     spread = psum.tile([P, 4, P], F32, name=f"spread{h}")
                     for i in range(4):
                         col = gate_cols[:, 4 * h + i : 4 * h + i + 1]
                         nc.tensor.transpose(spread[:, i, :], col.to_broadcast([P, P]), identity[:])
-                    nc.scalar.copy(gate_all[:, 4 * h : 4 * h + 4, :], spread[:])
+                    nc.scalar.copy(gate_all[:, :, 4 * h : 4 * h + 4], spread[:].rearrange("p i n -> p n i"))
         nc.sync.dma_start(
             w_codes[:].bitcast(I32), w1_words[0].rearrange("p n t -> p (n t)").bitcast(I32)
         )

@@ -17,7 +17,6 @@ ALU = mybir.AluOpType
 ACT = mybir.ActivationFunctionType
 
 P = 128
-PIECES = [(0, 256), (256, 640), (640, 1024)]
 
 
 def tile_picked_modres_linrelu_l_kernel(
@@ -32,14 +31,23 @@ def tile_picked_modres_linrelu_l_kernel(
         identity = keep.tile([P, P], F32, name="identity")
         make_identity(nc, identity[:])
         per = S // P
-        gate_cols = keep.tile([P, per], F32, name="gate_cols")
-        nc.scalar.dma_start(gate_cols[:], gate[0].rearrange("(p b) -> p b", b=per))
+        gate_cols = swap.tile([P, 2 * per], F32, name="gate_cols", offset=4096 - 32)
+        nc.sync.dma_start(gate_cols[:, :per], gate[0].rearrange("(p b) -> p b", b=per))
         w_scales = keep.tile([P, N], U8, name="w_scales", align_bytes=64)
         for q in range(4):
             nc.scalar.dma_start(
                 w_scales[32 * q : 32 * q + 4, :].bitcast(I32),
                 w1_scales[0, 4 * q : 4 * q + 4, :].bitcast(I32),
             )
+        gate_all = keep.tile([P, P, per], F32, name="gate_all")
+        for h in range(2):
+            spread = psum.tile([P, 4, P], F32, name=f"spread{h}")
+            for i in range(4):
+                col = gate_cols[:, 4 * h + i : 4 * h + i + 1]
+                nc.tensor.transpose(spread[:, i, :], col.to_broadcast([P, P]), identity[:])
+            move = nc.vector.tensor_copy if h else nc.scalar.copy
+            move(gate_all[:, :, 4 * h : 4 * h + 4], spread[:].rearrange("p i n -> p n i"))
+        gates = gate_all[:].rearrange("p n i -> p (n i)")
 
         offsets = keep.tile([P, S // 16], U16, name="offsets")
 
@@ -47,126 +55,82 @@ def tile_picked_modres_linrelu_l_kernel(
             return offsets[:, a // 16 : b // 16]
 
         rows = xT.rearrange("(p j) t -> p j t", j=4)
-        ahead = PIECES[:2]
-        quads = [keep.tile([P, (b - a) * 4], BF16, name=f"quads{a}", align_bytes=64) for a, b in ahead]
-        slots = [t[:].rearrange("p (n j) -> p n j", j=4) for t in quads]
-        fourth = [t[:, :, 3] for t in slots]
-        early = [keep.tile([P, 2, b - a], U32, name=f"early{a}") for a, b in ahead]
-        early_halves = [t[:].bitcast(BF16).rearrange("p u (n e) -> p u n e", e=2) for t in early]
-        nc.vector.memset(early[1][:], 0)
-        nc.scalar.copy(early[0][:], early[1][:, :, : PIECES[0][1]])
-        a2, b2 = PIECES[2]
-        flat = keep.tile([P, 4, b2 - a2], BF16, name="flat")
+        pieces = [(0, 256), (256, 512), (512, S)]
+        quads = {
+            a: swap.tile([P, (b - a) * 4], BF16, name=f"quads{a}", offset={0: 2048, 256: 0, 512: 4096}[a], align_bytes=64)
+            for a, b in pieces
+        }
+        slots = {a: t[:].rearrange("p (n j) -> p n j", j=4) for a, t in quads.items()}
+        by_vector = {0: pieces[:2], 1: pieces[:2], 2: pieces[1:2], 3: pieces[1:2]}
+        by_scalar = {0: pieces[2:], 1: pieces[2:], 2: [(0, 256), (512, S)], 3: [(0, 128), (128, 256), (512, S)]}
 
-        w_codes = keep.tile([P, N], U32, name="w_codes", align_bytes=64)
+        def slot(a, b, j):
+            start = max(p for p in slots if p <= a)
+            return slots[start][:, a - start : b - start, j]
+
         for j in (0, 2, 1, 3):
             plane = keep.tile([P, T], F32, name=f"plane{j}", align_bytes=256)
             nc.sync.dma_start(plane[:], rows[:, j, :])
             if j == 0:
                 nc.sync.dma_start(offsets[:], offs)
-            if j == 3:
-                nc.vector.tensor_copy(fourth[0], plane[:].indirect(entries(*PIECES[0])))
-                lent = keep.tile([P, PIECES[1][1] - PIECES[1][0]], BF16, name="lent")
-                nc.scalar.activation(lent[:], plane[:].indirect(entries(*PIECES[1])), ACT.Copy)
-                nc.vector.tensor_copy(fourth[1][:, :256], lent[:, :256])
-            elif j == 1:
-                for c in range(2):
-                    nc.gpsimd.tensor_copy(
-                        quads[c][:].bitcast(U32).rearrange("p (n u) -> p n u", u=2),
-                        early[c][:].rearrange("p u n -> p n u"),
-                    )
-                nc.vector.tensor_copy(slots[0][:, :, 1], plane[:].indirect(entries(*PIECES[0])))
-                lent_early = keep.tile([P, PIECES[1][1] - PIECES[1][0]], BF16, name="lent_early")
-                nc.scalar.activation(lent_early[:], plane[:].indirect(entries(*PIECES[1])), ACT.Copy)
-                nc.vector.tensor_copy(slots[1][:, :, 1], lent_early[:])
-            else:
-                for c, (a, b) in enumerate(ahead):
-                    nc.vector.tensor_copy(early_halves[c][:, j // 2, :, j % 2], plane[:].indirect(entries(a, b)))
-            nc.scalar.activation(flat[:, j, :], plane[:].indirect(entries(a2, b2)), ACT.Copy)
-            if j == 3:
-                nc.scalar.copy(fourth[1][:, 256:], lent[:, 256:])
-            if j == 0:
-                gate_all = keep.tile([P, P, per], F32, name="gate_all")
-                for h in range(2):
-                    spread = psum.tile([P, 4, P], F32, name=f"spread{h}")
-                    for i in range(4):
-                        col = gate_cols[:, 4 * h + i : 4 * h + i + 1]
-                        nc.tensor.transpose(spread[:, i, :], col.to_broadcast([P, P]), identity[:])
-                    nc.scalar.copy(gate_all[:, :, 4 * h : 4 * h + 4], spread[:].rearrange("p i n -> p n i"))
+            for a, b in by_vector[j]:
+                nc.vector.tensor_copy(slot(a, b, j), plane[:].indirect(entries(a, b)))
+            for a, b in by_scalar[j]:
+                nc.scalar.activation(slot(a, b, j), plane[:].indirect(entries(a, b)), ACT.Copy)
+        w_codes = keep.tile([P, N], U32, name="w_codes", align_bytes=64)
         nc.sync.dma_start(
             w_codes[:].bitcast(I32), w1_words[0].rearrange("p n t -> p (n t)").bitcast(I32)
         )
         stream = keep.tile([P, T], F32, name="stream", align_bytes=256)
         nc.sync.dma_start(stream[:], res)
-        gates = gate_all[:].rearrange("p n i -> p (n i)")
-
-        cut = 256
-        again = keep.tile([P, T], F32, name="again", tag="plane3", align_bytes=256)
+        again = swap.tile([P, T], F32, name="again", offset=8192, align_bytes=256)
         nc.sync.dma_start(again[:], res)
-        old = keep.tile([P, S], F32, name="old")
-        nc.scalar.activation(old[:, cut:768], stream[:].indirect(entries(cut, 768)), ACT.Copy)
 
-        def multiply(name, source, a, b, tag, held=False):
-            n = b - a
-            codes = keep.tile([P, n], U32, name=f"codes{name}", tag=tag, align_bytes=64)
-            if held:
-                scales = swap.tile([P, n], U8, name=f"scales{name}", offset=3200, align_bytes=64)
-            else:
-                scales = keep.tile([P, n], U8, name=f"scales{name}", align_bytes=64)
+        def multiply(a, b, codes, scales):
+            start = max(p for p in quads if p <= a)
+            source = quads[start][:, 4 * (a - start) : 4 * (b - start)]
             nc.vector.quantize_mx(out=codes[:].bitcast(FP8X4), scales=scales[:], in_=source)
-            acc = psum.tile([P, n], F32, name=f"acc{name}", tag={0: "turned", 896: "spread0"}.get(a, f"acc{name}"))
-            for lo in range(0, n, 256):
-                cols = slice(lo, min(lo + 256, n))
-                nc.tensor.matmul_mx(
-                    out=acc[:, cols],
-                    lhsT=w_codes[:].bitcast(FP8X4),
-                    lhsT_scale=w_scales[:],
-                    rhs=codes[:, cols].bitcast(FP8X4),
-                    rhs_scale=scales[:, cols],
-                    start=True,
-                    stop=True,
-                )
+            acc = psum.tile([P, b - a], F32, name=f"acc{a}")
+            nc.tensor.matmul_mx(
+                out=acc[:],
+                lhsT=w_codes[:].bitcast(FP8X4),
+                lhsT_scale=w_scales[:],
+                rhs=codes[:].bitcast(FP8X4),
+                rhs_scale=scales[:],
+                start=True,
+                stop=True,
+            )
             return acc
 
         def gated(update, acc, a, b):
             nc.vector.scalar_tensor_tensor(update, acc[:], 0.0, gates[:, a:b], ALU.max, ALU.mult)
 
-        def product(name, source, a, b, update, tag):
-            gated(update, multiply(name, source, a, b, tag), a, b)
+        def own(name, n, dtype):
+            return keep.tile([P, n], dtype, name=name, align_bytes=64)
 
-        a0, b0 = PIECES[0]
-        a1, b1 = PIECES[1]
-        mid = (a0 + b0) // 2
-        news = [keep.tile([P, b - a], F32, name=f"new{a}") for a, b in ahead]
-        updates = [
-            swap.tile([P, mid - a0], F32, name="update0", offset=3072, align_bytes=64),
-            keep.tile([P, b0 - mid], F32, name="update0b"),
-        ]
-        product(0, quads[0][:, : 4 * mid], a0, mid, updates[0][:], "codes0")
-        product(mid, quads[0][:, 4 * mid :], mid, b0, updates[1][:], "codes_ahead")
-        update = swap.tile([P, b1 - a1], F32, name="update1", offset=3520, align_bytes=64)
-        for (a, b), part in zip(((a0, mid), (mid, b0)), updates):
-            nc.vector.tensor_tensor(news[0][:, a:b], stream[:].indirect(entries(a, b)), part[:], ALU.add)
-        sums = [
-            multiply(a1, quads[1][:, :1024], a1, 512, "codes_ahead"),
-            multiply(512, quads[1][:, 1024:], 512, b1, "codes512", held=True),
-        ]
-        gated(update[:, :256], sums[0], a1, 512)
-        gated(update[:, 256:], sums[1], 512, b1)
-        nc.vector.tensor_tensor(news[1][:], old[:, a1:b1], update[:], ALU.add)
+        def lent(name, n, dtype, offset):
+            return swap.tile([P, n], dtype, name=name, offset=offset, align_bytes=64)
 
-        late = keep.tile([P, b2 - a2], F32, name="late")
-        nc.vector.tensor_copy(old[:, 768:], again[:].indirect(entries(768, b2)))
-        for a, b in ((640, 768), (768, 896), (896, 1024)):
-            woven = swap.tile([P, (b - a) * 4], BF16, name=f"quads{a}", offset={640: 2112, 768: 4992, 896: 3584}[a], align_bytes=64)
-            source = woven[:]
-            nc.vector.tensor_copy(
-                source.rearrange("p (c i t) -> p c t i", i=4, t=4),
-                flat[:, :, a - a2 : b - a2].rearrange("p t (c i) -> p c t i", i=4),
-            )
-            product(a, source, a, b, late[:, a - a2 : b - a2], f"codes{a}")
+        halves = ((0, 128), (128, 256))
+        sums = [multiply(a, b, own(f"codes{a}", 128, U32), own(f"scales{a}", 128, U8)) for a, b in halves]
+        second_sum = multiply(256, 512, lent("codes256", 256, U32, 2048), own("scales256", 256, U8))
+        first = lent("first", 256, F32, 512)
+        old = keep.tile([P, S], F32, name="old")
+        new = keep.tile([P, 512], F32, name="new")
+        for (a, b), acc in zip(halves, sums):
+            gated(first[:, a:b], acc, a, b)
+        for a, b in halves:
+            nc.vector.tensor_tensor(new[:, a:b], stream[:].indirect(entries(a, b)), first[:, a:b], ALU.add)
+        nc.scalar.activation(old[:, 256:512], stream[:].indirect(entries(256, 512)), ACT.Copy)
+        second = lent("second", 256, F32, 1024)
+        gated(second[:], second_sum, 256, 512)
+        late_sum = multiply(512, S, own("codes512", 512, U32), lent("scales512", 512, U8, 512))
+        nc.vector.tensor_tensor(new[:, 256:], old[:, 256:512], second[:], ALU.add)
+        nc.vector.tensor_copy(old[:, 512:], again[:].indirect(entries(512, S)))
+        third = lent("third", 512, F32, 8192)
+        gated(third[:], late_sum, 512, S)
 
-        for (a, b), new in zip(ahead, news):
-            nc.scalar.activation(stream[:].indirect(entries(a, b)), new[:], ACT.Copy)
-        nc.vector.tensor_tensor(stream[:].indirect(entries(a2, b2)), old[:, a2:b2], late[:], ALU.add)
+        for a, b in ((0, 256), (256, 512)):
+            nc.scalar.activation(stream[:].indirect(entries(a, b)), new[:, a:b], ACT.Copy)
+        nc.vector.tensor_tensor(stream[:].indirect(entries(512, S)), old[:, 512:], third[:], ALU.add)
         nc.sync.dma_start(out, stream[:])

@@ -31,7 +31,7 @@ def tile_picked_modres_linrelu_l_kernel(
         identity = keep.tile([P, P], F32, name="identity")
         make_identity(nc, identity[:])
         per = S // P
-        gate_cols = swap.tile([P, 2 * per], F32, name="gate_cols", offset=4096 - 32)
+        gate_cols = swap.tile([P, 512 + 2 * per], F32, name="gate_cols", offset=6144 - 32)
         nc.sync.dma_start(gate_cols[:, :per], gate[0].rearrange("(p b) -> p b", b=per))
         w_scales = keep.tile([P, N], U8, name="w_scales", align_bytes=64)
         for q in range(4):
@@ -55,14 +55,16 @@ def tile_picked_modres_linrelu_l_kernel(
             return offsets[:, a // 16 : b // 16]
 
         rows = xT.rearrange("(p j) t -> p j t", j=4)
-        pieces = [(0, 256), (256, 512), (512, S)]
+        pieces = [(0, 256), (256, 512), (512, 768)]
         quads = {
-            a: swap.tile([P, (b - a) * 4], BF16, name=f"quads{a}", offset={0: 2048, 256: 0, 512: 4096}[a], align_bytes=64)
+            a: swap.tile([P, (b - a) * 4], BF16, name=f"quads{a}", offset={0: 4096, 256: 2048, 512: 8192}[a], align_bytes=64)
             for a, b in pieces
         }
         slots = {a: t[:].rearrange("p (n j) -> p n j", j=4) for a, t in quads.items()}
         by_vector = {0: pieces[:2], 1: pieces[:2], 2: pieces[1:2], 3: pieces[1:2]}
-        by_scalar = {0: pieces[2:], 1: pieces[2:], 2: [(0, 256), (512, S)], 3: [(0, 128), (128, 256), (512, S)]}
+        by_scalar = {0: pieces[2:], 1: pieces[2:], 2: [(0, 256), (512, 768)], 3: [(0, 128), (128, 256), (512, 768)]}
+        pairs = swap.tile([P, 2, S - 768], U32, name="pairs", offset=6144)
+        pair_halves = pairs[:].bitcast(BF16).rearrange("p u (n e) -> p u n e", e=2)
 
         def slot(a, b, j):
             start = max(p for p in slots if p <= a)
@@ -77,30 +79,35 @@ def tile_picked_modres_linrelu_l_kernel(
                 nc.vector.tensor_copy(slot(a, b, j), plane[:].indirect(entries(a, b)))
             for a, b in by_scalar[j]:
                 nc.scalar.activation(slot(a, b, j), plane[:].indirect(entries(a, b)), ACT.Copy)
+            nc.scalar.activation(pair_halves[:, j // 2, :, j % 2], plane[:].indirect(entries(768, S)), ACT.Copy)
         w_codes = keep.tile([P, N], U32, name="w_codes", align_bytes=64)
         nc.sync.dma_start(
             w_codes[:].bitcast(I32), w1_words[0].rearrange("p n t -> p (n t)").bitcast(I32)
         )
         stream = keep.tile([P, T], F32, name="stream", align_bytes=256)
         nc.sync.dma_start(stream[:], res)
-        again = swap.tile([P, T], F32, name="again", offset=8192, align_bytes=256)
+        again = swap.tile([P, T], F32, name="again", offset=10240, align_bytes=256)
         nc.sync.dma_start(again[:], res)
 
-        def multiply(a, b, codes, scales):
+        def multiply(a, b, codes, scales, acc):
             start = max(p for p in quads if p <= a)
             source = quads[start][:, 4 * (a - start) : 4 * (b - start)]
             nc.vector.quantize_mx(out=codes[:].bitcast(FP8X4), scales=scales[:], in_=source)
-            acc = psum.tile([P, b - a], F32, name=f"acc{a}")
-            nc.tensor.matmul_mx(
-                out=acc[:],
-                lhsT=w_codes[:].bitcast(FP8X4),
-                lhsT_scale=w_scales[:],
-                rhs=codes[:].bitcast(FP8X4),
-                rhs_scale=scales[:],
-                start=True,
-                stop=True,
-            )
+            for lo in range(0, b - a, 256):
+                cols = slice(lo, min(lo + 256, b - a))
+                nc.tensor.matmul_mx(
+                    out=acc[:, cols],
+                    lhsT=w_codes[:].bitcast(FP8X4),
+                    lhsT_scale=w_scales[:],
+                    rhs=codes[:, cols].bitcast(FP8X4),
+                    rhs_scale=scales[:, cols],
+                    start=True,
+                    stop=True,
+                )
             return acc
+
+        def bank(name, n):
+            return psum.tile([P, n], F32, name=name)
 
         def gated(update, acc, a, b):
             nc.vector.scalar_tensor_tensor(update, acc[:], 0.0, gates[:, a:b], ALU.max, ALU.mult)
@@ -112,23 +119,29 @@ def tile_picked_modres_linrelu_l_kernel(
             return swap.tile([P, n], dtype, name=name, offset=offset, align_bytes=64)
 
         halves = ((0, 128), (128, 256))
-        sums = [multiply(a, b, own(f"codes{a}", 128, U32), own(f"scales{a}", 128, U8)) for a, b in halves]
-        second_sum = multiply(256, 512, lent("codes256", 256, U32, 2048), own("scales256", 256, U8))
-        first = lent("first", 256, F32, 512)
+        sums = [multiply(a, b, own(f"codes{a}", 128, U32), own(f"scales{a}", 128, U8), bank(f"acc{a}", 128)) for a, b in halves]
+        second_sum = multiply(256, 512, lent("codes256", 256, U32, 4096), own("scales256", 256, U8), bank("acc256", 256))
+        first = {0: lent("first0", 128, F32, 1984), 128: lent("first128", 128, F32, 3584)}
         old = keep.tile([P, S], F32, name="old")
         new = keep.tile([P, 512], F32, name="new")
         for (a, b), acc in zip(halves, sums):
-            gated(first[:, a:b], acc, a, b)
+            gated(first[a][:], acc, a, b)
         for a, b in halves:
-            nc.vector.tensor_tensor(new[:, a:b], stream[:].indirect(entries(a, b)), first[:, a:b], ALU.add)
+            nc.vector.tensor_tensor(new[:, a:b], stream[:].indirect(entries(a, b)), first[a][:], ALU.add)
         nc.scalar.activation(old[:, 256:512], stream[:].indirect(entries(256, 512)), ACT.Copy)
-        second = lent("second", 256, F32, 1024)
+        late_sums = [multiply(512, 768, own("codes512", 256, U32), lent("scales512", 256, U8, 2048), bank("acc512", 256))]
+        quads[768] = lent("quads768", 1024, BF16, 0)
+        nc.vector.tensor_copy(
+            quads[768][:].bitcast(U32).rearrange("p (n u) -> p n u", u=2), pairs[:].rearrange("p u n -> p n u")
+        )
+        second = lent("second", 256, F32, 2432)
+        third = own("third", 512, F32)
         gated(second[:], second_sum, 256, 512)
-        late_sum = multiply(512, S, own("codes512", 512, U32), lent("scales512", 512, U8, 512))
+        late_sums.append(multiply(768, S, own("codes768", 256, U32), own("scales768", 256, U8), bank("acc768", 256)))
         nc.vector.tensor_tensor(new[:, 256:], old[:, 256:512], second[:], ALU.add)
+        gated(third[:, :256], late_sums[0], 512, 768)
+        gated(third[:, 256:], late_sums[1], 768, S)
         nc.vector.tensor_copy(old[:, 512:], again[:].indirect(entries(512, S)))
-        third = lent("third", 512, F32, 8192)
-        gated(third[:], late_sum, 512, S)
 
         for a, b in ((0, 256), (256, 512)):
             nc.scalar.activation(stream[:].indirect(entries(a, b)), new[:, a:b], ACT.Copy)

@@ -126,9 +126,11 @@ def tile_picked_modres_linrelu_l_kernel(
         new = keep.tile([P, 512], F32, name="new")
         for (a, b), acc in zip(halves, sums):
             gated(first[a][:], acc, a, b)
-        for a, b in halves:
-            nc.vector.tensor_tensor(new[:, a:b], stream[:].indirect(entries(a, b)), first[a][:], ALU.add)
-        nc.scalar.activation(old[:, 256:512], stream[:].indirect(entries(256, 512)), ACT.Copy)
+        nc.vector.tensor_tensor(new[:, :128], stream[:].indirect(entries(0, 128)), first[0][:], ALU.add)
+        nc.vector.tensor_tensor(new[:, 128:192], stream[:].indirect(entries(128, 192)), first[128][:, :64], ALU.add)
+        for a, b in ((192, 256), (256, 512)):
+            nc.scalar.activation(old[:, a:b], stream[:].indirect(entries(a, b)), ACT.Copy)
+        nc.vector.tensor_tensor(new[:, 192:256], old[:, 192:256], first[128][:, 64:], ALU.add)
         late_sums = [multiply(512, 768, own("codes512", 256, U32), lent("scales512", 256, U8, 2048), bank("acc512", 256))]
         quads[768] = lent("quads768", 1024, BF16, 0)
         nc.vector.tensor_copy(

@@ -110,7 +110,7 @@ def tile_picked_modres_linrelu_l_kernel(
             return psum.tile([P, n], F32, name=name)
 
         def gated(update, acc, a, b):
-            nc.vector.scalar_tensor_tensor(update, acc[:], 0.0, gates[:, a:b], ALU.max, ALU.mult)
+            nc.vector.scalar_tensor_tensor(update, acc[:, :], 0.0, gates[:, a:b], ALU.max, ALU.mult)
 
         def own(name, n, dtype):
             return keep.tile([P, n], dtype, name=name, align_bytes=64)
@@ -121,29 +121,31 @@ def tile_picked_modres_linrelu_l_kernel(
         halves = ((0, 128), (128, 256))
         sums = [multiply(a, b, own(f"codes{a}", 128, U32), own(f"scales{a}", 128, U8), bank(f"acc{a}", 128)) for a, b in halves]
         second_sum = multiply(256, 512, lent("codes256", 256, U32, 4096), own("scales256", 256, U8), bank("acc256", 256))
-        first = {0: lent("first0", 128, F32, 1984), 128: lent("first128", 128, F32, 3584)}
+        fused = lent("fused", 160, F32, 1984)
+        plain = lent("plain", 96, F32, 3648)
         old = keep.tile([P, S], F32, name="old")
         new = keep.tile([P, 512], F32, name="new")
-        for (a, b), acc in zip(halves, sums):
-            gated(first[a][:], acc, a, b)
-        nc.vector.tensor_tensor(new[:, :128], stream[:].indirect(entries(0, 128)), first[0][:], ALU.add)
-        nc.vector.tensor_tensor(new[:, 128:192], stream[:].indirect(entries(128, 192)), first[128][:, :64], ALU.add)
-        for a, b in ((192, 256), (256, 512)):
+        gated(fused[:, :128], sums[0], 0, 128)
+        gated(fused[:, 128:], sums[1][:, :32], 128, 160)
+        gated(plain[:], sums[1][:, 32:], 160, 256)
+        nc.vector.tensor_tensor(new[:, :160], stream[:].indirect(entries(0, 160)), fused[:], ALU.add)
+        for a, b in ((160, 256), (256, 448)):
             nc.scalar.activation(old[:, a:b], stream[:].indirect(entries(a, b)), ACT.Copy)
-        nc.vector.tensor_tensor(new[:, 192:256], old[:, 192:256], first[128][:, 64:], ALU.add)
+        nc.vector.tensor_tensor(new[:, 160:256], old[:, 160:256], plain[:], ALU.add)
         late_sums = [multiply(512, 768, own("codes512", 256, U32), lent("scales512", 256, U8, 2048), bank("acc512", 256))]
         quads[768] = lent("quads768", 1024, BF16, 0)
         nc.vector.tensor_copy(
             quads[768][:].bitcast(U32).rearrange("p (n u) -> p n u", u=2), pairs[:].rearrange("p u n -> p n u")
         )
-        second = lent("second", 256, F32, 2432)
-        third = own("third", 512, F32)
+        second = lent("second", 256, F32, 2560)
         gated(second[:], second_sum, 256, 512)
         late_sums.append(multiply(768, S, own("codes768", 256, U32), own("scales768", 256, U8), bank("acc768", 256)))
-        nc.vector.tensor_tensor(new[:, 256:], old[:, 256:512], second[:], ALU.add)
+        nc.vector.tensor_tensor(new[:, 256:448], old[:, 256:448], second[:, :192], ALU.add)
+        nc.vector.tensor_tensor(new[:, 448:], again[:].indirect(entries(448, 512)), second[:, 192:], ALU.add)
+        nc.vector.tensor_copy(old[:, 512:], again[:].indirect(entries(512, S)))
+        third = lent("third", 512, F32, 3520)
         gated(third[:, :256], late_sums[0], 512, 768)
         gated(third[:, 256:], late_sums[1], 768, S)
-        nc.vector.tensor_copy(old[:, 512:], again[:].indirect(entries(512, S)))
 
         for a, b in ((0, 256), (256, 512)):
             nc.scalar.activation(stream[:].indirect(entries(a, b)), new[:, a:b], ACT.Copy)

@@ -31,8 +31,10 @@ def tile_picked_modres_linrelu_l_kernel(
         identity = keep.tile([P, P], F32, name="identity")
         make_identity(nc, identity[:])
         per = S // P
-        gate_cols = swap.tile([P, 512 + 2 * per], F32, name="gate_cols", offset=6144 - 32)
-        nc.sync.dma_start(gate_cols[:, :per], gate[0].rearrange("(p b) -> p b", b=per))
+        landing = swap.tile([P, 512 + 2 * per], F32, name="landing", offset=6144 - 32)
+        nc.scalar.dma_start(landing[:, :per], gate[0].rearrange("(p b) -> p b", b=per))
+        gate_cols = keep.tile([P, per], F32, name="gate_cols")
+        nc.scalar.copy(gate_cols[:], landing[:, :per])
         w_scales = keep.tile([P, N], U8, name="w_scales", align_bytes=64)
         for q in range(4):
             nc.scalar.dma_start(
@@ -45,8 +47,7 @@ def tile_picked_modres_linrelu_l_kernel(
             for i in range(4):
                 col = gate_cols[:, 4 * h + i : 4 * h + i + 1]
                 nc.tensor.transpose(spread[:, i, :], col.to_broadcast([P, P]), identity[:])
-            move = nc.vector.tensor_copy if h else nc.scalar.copy
-            move(gate_all[:, :, 4 * h : 4 * h + 4], spread[:].rearrange("p i n -> p n i"))
+            nc.vector.tensor_copy(gate_all[:, :, 4 * h : 4 * h + 4], spread[:].rearrange("p i n -> p n i"))
         gates = gate_all[:].rearrange("p n i -> p (n i)")
 
         offsets = keep.tile([P, S // 16], U16, name="offsets")

@@ -32,7 +32,12 @@ def tile_picked_modres_linrelu_l_kernel(
         make_identity(nc, identity[:])
         per = S // P
         landing = swap.tile([P, 512 + 2 * per], F32, name="landing", offset=6144 - 32)
-        nc.scalar.dma_start(landing[:, :per], gate[0].rearrange("(p b) -> p b", b=per))
+        rows = xT.rearrange("(p j) t -> p j t", j=4)
+        planes = {j: keep.tile([P, T], F32, name=f"plane{j}", align_bytes=256) for j in (0, 2, 1, 3)}
+        offsets = keep.tile([P, S // 16], U16, name="offsets")
+        nc.sync.dma_start(planes[0][:], rows[:, 0, :])
+        nc.sync.dma_start(offsets[:], offs)
+        nc.sync.dma_start(landing[:, :per], gate[0].rearrange("(p b) -> p b", b=per))
         gate_cols = keep.tile([P, per], F32, name="gate_cols")
         nc.scalar.copy(gate_cols[:], landing[:, :per])
         w_scales = keep.tile([P, N], U8, name="w_scales", align_bytes=64)
@@ -50,12 +55,9 @@ def tile_picked_modres_linrelu_l_kernel(
             nc.vector.tensor_copy(gate_all[:, :, 4 * h : 4 * h + 4], spread[:].rearrange("p i n -> p n i"))
         gates = gate_all[:].rearrange("p n i -> p (n i)")
 
-        offsets = keep.tile([P, S // 16], U16, name="offsets")
-
         def entries(a, b):
             return offsets[:, a // 16 : b // 16]
 
-        rows = xT.rearrange("(p j) t -> p j t", j=4)
         pieces = [(0, 256), (256, 512), (512, 768)]
         quads = {
             a: swap.tile([P, (b - a) * 4], BF16, name=f"quads{a}", offset={0: 4096, 256: 2048, 512: 8192}[a], align_bytes=64)
@@ -71,11 +73,9 @@ def tile_picked_modres_linrelu_l_kernel(
             start = max(p for p in slots if p <= a)
             return slots[start][:, a - start : b - start, j]
 
-        for j in (0, 2, 1, 3):
-            plane = keep.tile([P, T], F32, name=f"plane{j}", align_bytes=256)
-            nc.sync.dma_start(plane[:], rows[:, j, :])
-            if j == 0:
-                nc.sync.dma_start(offsets[:], offs)
+        for j, plane in planes.items():
+            if j:
+                nc.sync.dma_start(plane[:], rows[:, j, :])
             for a, b in by_vector[j]:
                 nc.vector.tensor_copy(slot(a, b, j), plane[:].indirect(entries(a, b)))
             for a, b in by_scalar[j]:

@@ -42,7 +42,7 @@ def tile_picked_modres_linrelu_l_kernel(
         nc.scalar.copy(gate_cols[:], landing[:, :per])
         w_scales = keep.tile([P, N], U8, name="w_scales", align_bytes=64)
         for q in range(4):
-            nc.scalar.dma_start(
+            nc.sync.dma_start(
                 w_scales[32 * q : 32 * q + 4, :].bitcast(I32),
                 w1_scales[0, 4 * q : 4 * q + 4, :].bitcast(I32),
             )

from contextlib import ExitStack

import concourse.mybir as mybir
from concourse.masks import make_identity

K, T, S, N = 512, 2048, 1024, 128
FLOPS = 2 * K * S * N

F32 = mybir.dt.float32
BF16 = mybir.dt.bfloat16
U32 = mybir.dt.uint32
I32 = mybir.dt.int32
U16 = mybir.dt.uint16
U8 = mybir.dt.uint8
FP8X4 = mybir.dt.float8_e4m3fn_x4
ALU = mybir.AluOpType
ACT = mybir.ActivationFunctionType

P = 128


def tile_picked_modres_linrelu_l_kernel(
    tc, xT, gate, res, w1_words, w1_scales, offs, out
):
    nc = tc.nc
    with ExitStack() as ctx:
        keep = ctx.enter_context(tc.tile_pool(name="keep", bufs=1))
        swap = ctx.enter_context(tc.tile_pool(name="swap", bufs=1))
        psum = ctx.enter_context(tc.psum_pool(name="psum", bufs=1))

        identity = keep.tile([P, P], F32, name="identity")
        make_identity(nc, identity[:])
        per = S // P
        landing = swap.tile([P, 512 + 2 * per], F32, name="landing", offset=6144 - 32)
        rows = xT.rearrange("(p j) t -> p j t", j=4)
        planes = {j: keep.tile([P, T], F32, name=f"plane{j}", align_bytes=256) for j in (0, 2, 1, 3)}
        offsets = keep.tile([P, S // 16], U16, name="offsets")
        nc.sync.dma_start(planes[0][:], rows[:, 0, :])
        nc.sync.dma_start(offsets[:], offs)
        nc.sync.dma_start(landing[:, :per], gate[0].rearrange("(p b) -> p b", b=per))
        gate_cols = keep.tile([P, per], F32, name="gate_cols")
        nc.scalar.copy(gate_cols[:], landing[:, :per])
        w_scales = keep.tile([P, N], U8, name="w_scales", align_bytes=64)
        for q in range(4):
            nc.sync.dma_start(
                w_scales[32 * q : 32 * q + 4, :].bitcast(I32),
                w1_scales[0, 4 * q : 4 * q + 4, :].bitcast(I32),
            )
        gate_all = keep.tile([P, P, per], F32, name="gate_all")
        for h in range(2):
            spread = psum.tile([P, 4, P], F32, name=f"spread{h}")
            for i in range(4):
                col = gate_cols[:, 4 * h + i : 4 * h + i + 1]
                nc.tensor.transpose(spread[:, i, :], col.to_broadcast([P, P]), identity[:])
            nc.vector.tensor_copy(gate_all[:, :, 4 * h : 4 * h + 4], spread[:].rearrange("p i n -> p n i"))
        gates = gate_all[:].rearrange("p n i -> p (n i)")

        def entries(a, b):
            return offsets[:, a // 16 : b // 16]

        pieces = [(0, 256), (256, 512), (512, 768)]
        quads = {
            a: swap.tile([P, (b - a) * 4], BF16, name=f"quads{a}", offset={0: 4096, 256: 2048, 512: 8192}[a], align_bytes=64)
            for a, b in pieces
        }
        slots = {a: t[:].rearrange("p (n j) -> p n j", j=4) for a, t in quads.items()}
        by_vector = {0: pieces[:2], 1: pieces[:2], 2: pieces[1:2], 3: pieces[1:2]}
        by_scalar = {0: pieces[2:], 1: pieces[2:], 2: [(0, 256), (512, 768)], 3: [(0, 128), (128, 256), (512, 768)]}
        pairs = swap.tile([P, 2, S - 768], U32, name="pairs", offset=6144)
        pair_halves = pairs[:].bitcast(BF16).rearrange("p u (n e) -> p u n e", e=2)

        def slot(a, b, j):
            start = max(p for p in slots if p <= a)
            return slots[start][:, a - start : b - start, j]

        for j, plane in planes.items():
            if j:
                nc.sync.dma_start(plane[:], rows[:, j, :])
            for a, b in by_vector[j]:
                nc.vector.tensor_copy(slot(a, b, j), plane[:].indirect(entries(a, b)))
            for a, b in by_scalar[j]:
                nc.scalar.activation(slot(a, b, j), plane[:].indirect(entries(a, b)), ACT.Copy)
            nc.scalar.activation(pair_halves[:, j // 2, :, j % 2], plane[:].indirect(entries(768, S)), ACT.Copy)
        w_codes = keep.tile([P, N], U32, name="w_codes", align_bytes=64)
        nc.sync.dma_start(
            w_codes[:].bitcast(I32), w1_words[0].rearrange("p n t -> p (n t)").bitcast(I32)
        )
        stream = keep.tile([P, T], F32, name="stream", align_bytes=256)
        nc.sync.dma_start(stream[:], res)
        again = swap.tile([P, T], F32, name="again", offset=10240, align_bytes=256)
        nc.sync.dma_start(again[:], res)

        def multiply(a, b, codes, scales, acc):
            start = max(p for p in quads if p <= a)
            source = quads[start][:, 4 * (a - start) : 4 * (b - start)]
            nc.vector.quantize_mx(out=codes[:].bitcast(FP8X4), scales=scales[:], in_=source)
            for lo in range(0, b - a, 256):
                cols = slice(lo, min(lo + 256, b - a))
                nc.tensor.matmul_mx(
                    out=acc[:, cols],
                    lhsT=w_codes[:].bitcast(FP8X4),
                    lhsT_scale=w_scales[:],
                    rhs=codes[:, cols].bitcast(FP8X4),
                    rhs_scale=scales[:, cols],
                    start=True,
                    stop=True,
                )
            return acc

        def bank(name, n):
            return psum.tile([P, n], F32, name=name)

        def gated(update, acc, a, b):
            nc.vector.scalar_tensor_tensor(update, acc[:, :], 0.0, gates[:, a:b], ALU.max, ALU.mult)

        def own(name, n, dtype):
            return keep.tile([P, n], dtype, name=name, align_bytes=64)

        def lent(name, n, dtype, offset):
            return swap.tile([P, n], dtype, name=name, offset=offset, align_bytes=64)

        halves = ((0, 128), (128, 256))
        sums = [multiply(a, b, own(f"codes{a}", 128, U32), own(f"scales{a}", 128, U8), bank(f"acc{a}", 128)) for a, b in halves]
        second_sum = multiply(256, 512, lent("codes256", 256, U32, 4096), own("scales256", 256, U8), bank("acc256", 256))
        fused = lent("fused", 160, F32, 1984)
        plain = lent("plain", 96, F32, 3648)
        old = keep.tile([P, S], F32, name="old")
        new = keep.tile([P, 512], F32, name="new")
        gated(fused[:, :128], sums[0], 0, 128)
        gated(fused[:, 128:], sums[1][:, :32], 128, 160)
        gated(plain[:], sums[1][:, 32:], 160, 256)
        nc.vector.tensor_tensor(new[:, :160], stream[:].indirect(entries(0, 160)), fused[:], ALU.add)
        for a, b in ((160, 256), (256, 448)):
            nc.scalar.activation(old[:, a:b], stream[:].indirect(entries(a, b)), ACT.Copy)
        nc.vector.tensor_tensor(new[:, 160:256], old[:, 160:256], plain[:], ALU.add)
        late_sums = [multiply(512, 768, own("codes512", 256, U32), lent("scales512", 256, U8, 2048), bank("acc512", 256))]
        quads[768] = lent("quads768", 1024, BF16, 0)
        nc.vector.tensor_copy(
            quads[768][:].bitcast(U32).rearrange("p (n u) -> p n u", u=2), pairs[:].rearrange("p u n -> p n u")
        )
        second = lent("second", 256, F32, 2560)
        gated(second[:], second_sum, 256, 512)
        late_sums.append(multiply(768, S, own("codes768", 256, U32), own("scales768", 256, U8), bank("acc768", 256)))
        nc.vector.tensor_tensor(new[:, 256:448], old[:, 256:448], second[:, :192], ALU.add)
        nc.vector.tensor_tensor(new[:, 448:], again[:].indirect(entries(448, 512)), second[:, 192:], ALU.add)
        nc.vector.tensor_copy(old[:, 512:], again[:].indirect(entries(512, S)))
        third = lent("third", 512, F32, 3520)
        gated(third[:, :256], late_sums[0], 512, 768)
        gated(third[:, 256:], late_sums[1], 768, S)

        for a, b in ((0, 256), (256, 512)):
            nc.scalar.activation(stream[:].indirect(entries(a, b)), new[:, a:b], ACT.Copy)
        nc.vector.tensor_tensor(stream[:].indirect(entries(512, S)), old[:, 512:], third[:], ALU.add)
        nc.sync.dma_start(out, stream[:])
